import numpy as np
import ml_dtypes


def mxq(x, axis, fmt="e4m3"):
    dtype, down = {"e4m3": (ml_dtypes.float8_e4m3fn, 7), "e5m2": (ml_dtypes.float8_e5m2, 14)}[fmt]
    v = np.moveaxis(np.asarray(x, np.float32).astype(ml_dtypes.bfloat16).astype(np.float64), axis, -1)
    blocks = v.reshape(v.shape[:-1] + (-1, 32))
    amax = np.abs(blocks).max(-1, keepdims=True)
    byte = np.maximum(np.where(amax > 0, np.frexp(amax)[1] - 1 + 127, 0) - down, 1)
    scale = np.exp2(byte - 127.0)
    codes = (blocks / scale).astype(np.float32).astype(dtype).astype(np.float64)
    return np.moveaxis((codes * scale).reshape(v.shape), -1, axis)


WIDE = False


def mx_kscale(k):
    if not WIDE:
        return np.ones(k)
    levels = np.array([10, -10, 5, -5, 0])
    if k % 512:
        return np.exp2(np.random.permutation(np.resize(levels, k // 32))).repeat(32)
    a = np.empty((k // 512, 16))
    for p in range(k // 512):
        a[p, :8] = np.random.permutation(np.resize(levels, 8))
        for g in range(8):
            far = levels[np.abs(levels - a[p, g]) >= 10]
            a[p, g + 8] = far[np.random.randint(len(far))]
    return np.exp2(a.ravel()).repeat(32)


def f64(x):
    return np.asarray(x).astype(np.float64)


def striped(idx):
    return np.tile(idx.reshape(-1, 16).T, (8, 1)).astype(np.uint16)


def unstriped(offs):
    return offs[:16].T.reshape(-1).astype(np.int64)


def striped8(idx):
    return np.concatenate([x.reshape(-1, 16).T for x in idx]).astype(np.uint16)


def runs(offs, k):
    lists = np.stack([offs[16 * r : 16 * r + 16].T.reshape(-1) for r in range(8)]).astype(np.int64)
    return lists[np.arange(k) % 512 // 64]


def pack_weight(w):
    k, n = w.shape
    w = f64(np.asarray(w, np.float32).astype(ml_dtypes.bfloat16)).reshape(k // 32, 32, n)
    amax = np.abs(w).max(1)
    byte = np.clip(np.where(amax > 0, np.frexp(amax)[1] - 1 + 127 - 7, 1), 1, 254)
    scaled = (w * np.exp2(127.0 - byte)[:, None, :]).reshape(k, n).astype(np.float32)
    words = np.ascontiguousarray(scaled.reshape(k // 512, 128, 4, n).transpose(0, 1, 3, 2)).astype(ml_dtypes.float8_e4m3fn).view(np.uint8)
    return words, np.ascontiguousarray(byte.astype(np.uint8).reshape(k // 512, 16, n))


def unpack_weight(words, scales):
    g, p, n, _ = words.shape
    vals = np.ascontiguousarray(words).view(ml_dtypes.float8_e4m3fn).astype(np.float64) * np.repeat(np.exp2(scales.astype(np.float64) - 127.0), 8, axis=1)[..., None]
    return vals.transpose(0, 1, 3, 2).reshape(g * 512, n)


K, T, S, V, N, H = 512, 2048, 512, 256, 512, 512


def setup_inputs():
    n = np.random.standard_normal
    s = mx_kscale(K)[:, None]
    u = mx_kscale(H)
    packed_xT = pack_weight(n((K, T)) * s)
    return {
        "x_words": packed_xT[0],
        "x_scales": packed_xT[1],
        "w1": (n((K, H)) / np.sqrt(K) / s * u).astype(np.float32),
        "fr1": np.repeat(np.random.uniform(0, 1, (8, V)), 64, axis=0).astype(np.float32),
        "fr2": np.repeat(np.random.uniform(0, 1, (8, V)), 64, axis=0).astype(np.float32),
        "w2": (n((H, N)) / np.sqrt(H) / u[:, None]).astype(np.float32),
        "offs": striped(np.random.permutation(T)[:S]),
        "l1": striped8(np.stack([np.random.permutation(S)[:V] for _ in range(8)])),
        "r1": striped8(np.stack([np.random.permutation(S)[:V] for _ in range(8)])),
        "l2": striped8(np.stack([np.random.permutation(S)[:V] for _ in range(8)])),
        "r2": striped8(np.stack([np.random.permutation(S)[:V] for _ in range(8)])),
    }


def reference(x_words, x_scales, w1, fr1, fr2, w2, offs, l1, r1, l2, r2):
    xq = unpack_weight(x_words, x_scales)[:, unstriped(offs)]
    y = mxq(f64(w1), 0, "e4m3").T @ xq
    q1 = y[np.arange(H)[:, None], runs(r1, H)]
    q2 = y[np.arange(H)[:, None], runs(r2, H)]
    z = np.maximum(q1 + f64(fr1) * (y[np.arange(H)[:, None], runs(l1, H)] - q1), q2 + f64(fr2) * (y[np.arange(H)[:, None], runs(l2, H)] - q2))
    return mxq(f64(w2), 0, "e4m3").T @ mxq(z, 0, "e4m3")

@@ -1,0 +1,160 @@
+from contextlib import ExitStack
+
+import concourse.mybir as mybir
+from concourse.masks import make_identity
+
+K, T, S, V, N, H = 512, 2048, 512, 256, 512, 512
+FLOPS = 2 * K * H * S + 2 * H * N * V
+
+F32 = mybir.dt.float32
+BF16 = mybir.dt.bfloat16
+I32 = mybir.dt.int32
+U32 = mybir.dt.uint32
+U16 = mybir.dt.uint16
+U8 = mybir.dt.uint8
+FP8X4 = mybir.dt.float8_e4m3fn_x4
+ALU = mybir.AluOpType
+ACT = mybir.ActivationFunctionType
+
+P = 128
+PACK = 4
+BANK = 512
+
+
+def tile_picked_roial_none_p_kernel(tc, x_words, x_scales, w1, fr1, fr2, w2, offs, l1, r1, l2, r2, out):
+    nc = tc.nc
+    with ExitStack() as ctx:
+        keep = ctx.enter_context(tc.tile_pool(name="keep", bufs=1))
+        psum = ctx.enter_context(tc.psum_pool(name="psum", bufs=1))
+
+        def bank(b, name):
+            return psum.tile([P, BANK], F32, name=name, tag=f"bank{b}")
+
+        def load_list(name, src):
+            lt = keep.tile([P, src.shape[1]], U16, name="list_" + name)
+            nc.sync.dma_start(lt[:], src)
+            return lt
+
+        def load_share(name, src):
+            f = keep.tile([P, V], F32, name=name)
+            nc.sync.dma_start(f[:], src.rearrange("(p j) v -> p j v", j=PACK)[:, 0, :])
+            return f
+
+        def load_weight_half(name, w, h):
+            raw = keep.tile([P, PACK, 256], F32, name=f"{name}raw{h}", tag=f"wraw{h}")
+            nc.sync.dma_start(raw[:], w.rearrange("(p j) c -> p j c", j=PACK)[:, :, 256 * h : 256 * (h + 1)])
+            return raw
+
+        def deal(copy, grouped, raw, h, lo, hi):
+            copy(
+                grouped[:, :, 64 * h + lo : 64 * h + hi, :].rearrange("p t m j -> p m j t"),
+                raw[:, :, PACK * lo : PACK * hi].rearrange("p j (m t) -> p m j t", t=PACK),
+            )
+
+        def add_transposed(dst, parts):
+            for i, part in enumerate(parts):
+                nc.tensor.matmul(dst, part, ident[:], start=(i == 0), stop=(i == len(parts) - 1), is_transpose=True)
+
+        offs_t = load_list("offs", offs)
+        xw = keep.tile([P, T], I32, name="xw", align_bytes=64)
+        nc.sync.dma_start(xw[:], x_words[0].rearrange("p n t -> p (n t)").bitcast(I32))
+        xs = keep.tile([P, T], U8, name="xs", align_bytes=64)
+        nc.vector.memset(xs[:].bitcast(I32), 0)
+        for q in range(4):
+            nc.sync.dma_start(xs[32 * q : 32 * q + 4, :].bitcast(I32), x_scales[0, 4 * q : 4 * q + 4, :].bitcast(I32))
+        w1raw = [load_weight_half("w1", w1, h) for h in range(2)]
+        f1 = load_share("f1", fr1)
+        l1_t = load_list("l1", l1)
+        r1_t = load_list("r1", r1)
+        f2 = load_share("f2", fr2)
+        l2_t = load_list("l2", l2)
+        r2_t = load_list("r2", r2)
+
+        ident = keep.tile([P, P], F32, name="ident")
+        make_identity(nc, ident[:])
+
+        xq_w = keep.tile([P, S], U32, name="xq_w", align_bytes=64)
+        nc.vector.tensor_copy(xq_w[:], xw[:].bitcast(U32).indirect(offs_t[:]))
+        xq_s = keep.tile([P, S], U8, name="xq_s", align_bytes=64)
+        nc.vector.tensor_copy(xq_s[:], xs[:].indirect(offs_t[:]))
+        w1g = keep.tile([P, PACK, P, PACK], BF16, name="w1g", align_bytes=64)
+        deal(nc.scalar.copy, w1g, w1raw[0], 0, 0, 64)
+        deal(nc.vector.tensor_copy, w1g, w1raw[1], 1, 0, 64)
+
+        ys = []
+        for t in range(PACK):
+            wc = keep.tile([P, P], U32, name=f"w1c{t}", align_bytes=64)
+            ws = keep.tile([P, P], U8, name=f"w1s{t}", align_bytes=64)
+            nc.vector.quantize_mx(wc[:].bitcast(FP8X4), ws[:], w1g[:, t].rearrange("p m j -> p (m j)"))
+            y = keep.tile([P, S], F32, name=f"y{t}")
+            if t == 0:
+                pieces = ((4, slice(0, 256), nc.scalar.copy), (0, slice(256, 512), nc.vector.tensor_copy))
+            else:
+                pieces = ((t, slice(0, S), nc.scalar.copy),)
+            for b, cols, copy in pieces:
+                acc = bank(b, f"yacc{t}_{b}")
+                nc.tensor.matmul_mx(acc[:, cols], wc[:].bitcast(FP8X4), ws[:], xq_w[:, cols].bitcast(FP8X4), xq_s[:, cols], start=True, stop=True)
+                copy(y[:, cols], acc[:, cols])
+            ys.append(y)
+
+        c1 = keep.tile([P, V], F32, name="c1")
+        nc.vector.tensor_scalar(c1[:], f1[:], -1.0, 1.0, ALU.mult, ALU.add)
+        nf2 = keep.tile([P, V], F32, name="nf2")
+        nc.vector.tensor_scalar(nf2[:], f2[:], -1.0, None, ALU.mult)
+        nc2 = keep.tile([P, V], F32, name="nc2")
+        nc.vector.tensor_scalar(nc2[:], f2[:], -1.0, None, ALU.add)
+        terms = ((l1_t, f1), (r1_t, c1), (l2_t, nf2), (r2_t, nc2))
+
+        w2g = keep.tile([P, PACK, P, PACK], BF16, name="w2g", align_bytes=64)
+        w2raw = [load_weight_half("w2", w2, h) for h in range(2)]
+        w2c = keep.tile([P, N], U32, name="w2c", align_bytes=64)
+        w2s = keep.tile([P, N], U8, name="w2s", align_bytes=64)
+
+        zacc = [bank(2 + h, f"zacc{h}") for h in range(2)]
+        units = ((0, 0, 2), (1, 0, 2), (2, 0, 2), (3, 0, 1), (3, 1, 2))
+        for u, (t, h0, h1) in enumerate(units):
+            cols = slice(P * h0, P * h1)
+            width = P * (h1 - h0)
+            gs = []
+            for i, (lst, share) in enumerate(terms):
+                gt = keep.tile([P, width], F32, name=f"g{u}_{i}")
+                nc.vector.tensor_tensor(gt[:], ys[t][:].indirect(lst[:, 8 * h0 : 8 * h1]), share[:, cols], ALU.mult)
+                gs.append(gt)
+            sacc = bank(5 - u % 2, f"sacc{u}")
+            dacc = bank(6 + u % 2, f"dacc{u}")
+            blocks = [slice(P * i, P * (i + 1)) for i in range(h1 - h0)]
+            for blk in blocks:
+                add_transposed(sacc[:, blk], [g[:, blk] for g in gs[:2]])
+            first = keep.tile([P, width], F32, name=f"first{u}")
+            nc.scalar.copy(first[:], sacc[:, :width])
+            for blk in blocks:
+                add_transposed(dacc[:, blk], [g[:, blk] for g in gs])
+            rise = keep.tile([P, width], F32, name=f"rise{u}")
+            nc.scalar.activation(rise[:], dacc[:, :width], ACT.Relu, scale=-1.0)
+            for i, blk in enumerate(blocks):
+                add_transposed(zacc[h0 + i][:, P * t : P * (t + 1)], [first[:, blk], rise[:, blk]])
+            if u < 2:
+                deal(nc.scalar.copy, w2g, w2raw[u], u, 0, 32)
+                deal(nc.scalar.copy, w2g, w2raw[u], u, 32, 64)
+
+        nc.vector.quantize_mx(w2c[:].bitcast(FP8X4), w2s[:], w2g[:].rearrange("p t m j -> p (t m j)"))
+
+        outv = out.rearrange("(p t) v -> p t v", t=PACK)
+        for h, zcopy in ((0, nc.vector.tensor_copy), (1, nc.scalar.copy)):
+            z = keep.tile([P, P, PACK], BF16, name=f"z{h}", align_bytes=64)
+            zcopy(z[:], zacc[h][:].rearrange("p (t v) -> p v t", t=PACK))
+            zc = keep.tile([P, P], U32, name=f"zc{h}", align_bytes=64)
+            zs = keep.tile([P, P], U8, name=f"zs{h}", align_bytes=64)
+            nc.vector.quantize_mx(zc[:].bitcast(FP8X4), zs[:], z[:].rearrange("p v t -> p (v t)"))
+            res = keep.tile([P, PACK, P], F32, name=f"res{h}")
+            if h == 0:
+                pieces = ((0, 0, 4, nc.scalar.copy),)
+            else:
+                pieces = ((1, 0, 2, nc.scalar.copy), (4, 2, 4, nc.vector.tensor_copy))
+            for b, t0, t1, copy in pieces:
+                acc = bank(b, f"oacc{h}_{b}")
+                for t in range(t0, t1):
+                    cols = slice(P * t, P * (t + 1))
+                    nc.tensor.matmul_mx(acc[:, cols], w2c[:, cols].bitcast(FP8X4), w2s[:, cols], zc[:].bitcast(FP8X4), zs[:], start=True, stop=True)
+                copy(res[:, t0:t1, :], acc[:, P * t0 : P * t1].rearrange("p (t v) -> p t v", v=P))
+            nc.sync.dma_start(outv[:, :, P * h : P * (h + 1)], res[:])

@@ -51,35 +51,33 @@ def tile_picked_roial_none_p_kernel(tc, x_words, x_scales, w1, fr1, fr2, w2, off
                 raw[:, :, PACK * lo : PACK * hi].rearrange("p j (m t) -> p m j t", t=PACK),
             )
 
-        def add_transposed(dst, parts):
-            for i, part in enumerate(parts):
-                nc.tensor.matmul(dst, part, ident[:], start=(i == 0), stop=(i == len(parts) - 1), is_transpose=True)
-
         offs_t = load_list("offs", offs)
-        xw = keep.tile([P, T], I32, name="xw", align_bytes=64)
-        nc.sync.dma_start(xw[:], x_words[0].rearrange("p n t -> p (n t)").bitcast(I32))
+        w1raw = [load_weight_half("w1", w1, 0)]
+        l1_t = load_list("l1", l1)
+        r1_t = load_list("r1", r1)
         xs = keep.tile([P, T], U8, name="xs", align_bytes=64)
         nc.vector.memset(xs[:].bitcast(I32), 0)
         for q in range(4):
             nc.sync.dma_start(xs[32 * q : 32 * q + 4, :].bitcast(I32), x_scales[0, 4 * q : 4 * q + 4, :].bitcast(I32))
-        w1raw = [load_weight_half("w1", w1, h) for h in range(2)]
-        f1 = load_share("f1", fr1)
-        l1_t = load_list("l1", l1)
-        r1_t = load_list("r1", r1)
-        f2 = load_share("f2", fr2)
+        xw = keep.tile([P, T], I32, name="xw", align_bytes=64)
+        nc.sync.dma_start(xw[:], x_words[0].rearrange("p n t -> p (n t)").bitcast(I32))
+        w1raw.append(load_weight_half("w1", w1, 1))
         l2_t = load_list("l2", l2)
         r2_t = load_list("r2", r2)
+        f1 = load_share("f1", fr1)
+        f2 = load_share("f2", fr2)
 
         ident = keep.tile([P, P], F32, name="ident")
         make_identity(nc, ident[:])
 
-        xq_w = keep.tile([P, S], U32, name="xq_w", align_bytes=64)
-        nc.vector.tensor_copy(xq_w[:], xw[:].bitcast(U32).indirect(offs_t[:]))
         xq_s = keep.tile([P, S], U8, name="xq_s", align_bytes=64)
         nc.vector.tensor_copy(xq_s[:], xs[:].indirect(offs_t[:]))
+        xq_w = keep.tile([P, S], U32, name="xq_w", align_bytes=64)
+        nc.vector.tensor_copy(xq_w[:], xw[:].bitcast(U32).indirect(offs_t[:]))
         w1g = keep.tile([P, PACK, P, PACK], BF16, name="w1g", align_bytes=64)
         deal(nc.scalar.copy, w1g, w1raw[0], 0, 0, 64)
-        deal(nc.vector.tensor_copy, w1g, w1raw[1], 1, 0, 64)
+        deal(nc.vector.tensor_copy, w1g, w1raw[1], 1, 0, 40)
+        deal(nc.scalar.copy, w1g, w1raw[1], 1, 40, 64)
 
         ys = []
         for t in range(PACK):
@@ -110,32 +108,57 @@ def tile_picked_roial_none_p_kernel(tc, x_words, x_scales, w1, fr1, fr2, w2, off
         w2c = keep.tile([P, N], U32, name="w2c", align_bytes=64)
         w2s = keep.tile([P, N], U8, name="w2s", align_bytes=64)
 
-        zacc = [bank(2 + h, f"zacc{h}") for h in range(2)]
+        zacc = [bank(4, "zacc0"), bank(0, "zacc1")]
         units = ((0, 0, 2), (1, 0, 2), (2, 0, 2), (3, 0, 1), (3, 1, 2))
+
+        def gather(u, i):
+            t, h0, h1 = units[u]
+            lst, share = terms[i]
+            g = keep.tile([P, P * (h1 - h0)], F32, name=f"g{u}_{i}")
+            nc.vector.tensor_tensor(g[:], ys[t][:].indirect(lst[:, 8 * h0 : 8 * h1]), share[:, P * h0 : P * h1], ALU.mult)
+            return [g[:, P * b : P * (b + 1)] for b in range(h1 - h0)]
+
+        def turn(dst, src, start, stop):
+            nc.tensor.matmul(dst, src, ident[:], start=start, stop=stop, is_transpose=True)
+
+        def turn_back(t, h0, first, rise):
+            for b in range(len(rise)):
+                dst = zacc[h0 + b][:, P * t : P * (t + 1)]
+                turn(dst, first[:, P * b : P * (b + 1)], True, False)
+                turn(dst, rise[b][:], False, True)
+
+        pending = None
         for u, (t, h0, h1) in enumerate(units):
-            cols = slice(P * h0, P * h1)
-            width = P * (h1 - h0)
-            gs = []
-            for i, (lst, share) in enumerate(terms):
-                gt = keep.tile([P, width], F32, name=f"g{u}_{i}")
-                nc.vector.tensor_tensor(gt[:], ys[t][:].indirect(lst[:, 8 * h0 : 8 * h1]), share[:, cols], ALU.mult)
-                gs.append(gt)
-            sacc = bank(5 - u % 2, f"sacc{u}")
-            dacc = bank(6 + u % 2, f"dacc{u}")
-            blocks = [slice(P * i, P * (i + 1)) for i in range(h1 - h0)]
-            for blk in blocks:
-                add_transposed(sacc[:, blk], [g[:, blk] for g in gs[:2]])
-            first = keep.tile([P, width], F32, name=f"first{u}")
-            nc.scalar.copy(first[:], sacc[:, :width])
-            for blk in blocks:
-                add_transposed(dacc[:, blk], [g[:, blk] for g in gs])
-            rise = keep.tile([P, width], F32, name=f"rise{u}")
-            nc.scalar.activation(rise[:], dacc[:, :width], ACT.Relu, scale=-1.0)
-            for i, blk in enumerate(blocks):
-                add_transposed(zacc[h0 + i][:, P * t : P * (t + 1)], [first[:, blk], rise[:, blk]])
+            blocks = range(h1 - h0)
+            g1 = gather(u, 0)
+            g2 = gather(u, 1)
+            sacc = bank(5, f"sacc{u}")
+            for b in blocks:
+                turn(sacc[:, P * b : P * (b + 1)], g1[b], True, False)
+                turn(sacc[:, P * b : P * (b + 1)], g2[b], False, True)
+            first = keep.tile([P, P * len(blocks)], F32, name=f"first{u}")
+            nc.scalar.copy(first[:], sacc[:, : P * len(blocks)])
+            dacc = [bank((6, 2)[u % 2] + b, f"dacc{u}_{b}") for b in blocks]
+            for b in blocks:
+                turn(dacc[b][:, :P], g1[b], True, False)
+                turn(dacc[b][:, :P], g2[b], False, False)
+            if pending is not None:
+                turn_back(*pending)
+            n3 = gather(u, 2)
+            for b in blocks:
+                turn(dacc[b][:, :P], n3[b], False, False)
+            n4 = gather(u, 3)
+            rise = []
+            for b in blocks:
+                turn(dacc[b][:, :P], n4[b], False, True)
+                r = keep.tile([P, P], F32, name=f"rise{u}_{b}")
+                nc.scalar.activation(r[:], dacc[b][:, :P], ACT.Relu, scale=-1.0)
+                rise.append(r)
+            pending = (t, h0, first, rise)
             if u < 2:
                 deal(nc.scalar.copy, w2g, w2raw[u], u, 0, 32)
                 deal(nc.scalar.copy, w2g, w2raw[u], u, 32, 64)
+        turn_back(*pending)
 
         nc.vector.quantize_mx(w2c[:].bitcast(FP8X4), w2s[:], w2g[:].rearrange("p t m j -> p (t m j)"))
 
@@ -148,13 +171,13 @@ def tile_picked_roial_none_p_kernel(tc, x_words, x_scales, w1, fr1, fr2, w2, off
             nc.vector.quantize_mx(zc[:].bitcast(FP8X4), zs[:], z[:].rearrange("p v t -> p (v t)"))
             res = keep.tile([P, PACK, P], F32, name=f"res{h}")
             if h == 0:
-                pieces = ((0, 0, 4, nc.scalar.copy),)
+                pieces = ((1, 0, 4, nc.scalar.copy, nc.sync),)
             else:
-                pieces = ((1, 0, 2, nc.scalar.copy), (4, 2, 4, nc.vector.tensor_copy))
-            for b, t0, t1, copy in pieces:
+                pieces = ((3, 0, 2, nc.scalar.copy, nc.scalar), (7, 2, 4, nc.vector.tensor_copy, nc.sync))
+            for b, t0, t1, copy, queue in pieces:
                 acc = bank(b, f"oacc{h}_{b}")
                 for t in range(t0, t1):
                     cols = slice(P * t, P * (t + 1))
                     nc.tensor.matmul_mx(acc[:, cols], w2c[:, cols].bitcast(FP8X4), w2s[:, cols], zc[:].bitcast(FP8X4), zs[:], start=True, stop=True)
                 copy(res[:, t0:t1, :], acc[:, P * t0 : P * t1].rearrange("p (t v) -> p t v", v=P))
-            nc.sync.dma_start(outv[:, :, P * h : P * (h + 1)], res[:])
+                queue.dma_start(outv[:, t0:t1, P * h : P * (h + 1)], res[:, t0:t1, :])

@@ -40,140 +40,200 @@ def tile_picked_roial_none_p_kernel(tc, x_words, x_scales, w1, fr1, fr2, w2, off
             nc.sync.dma_start(f[:], src.rearrange("(p j) v -> p j v", j=PACK)[:, 0, :])
             return f
 
-        def load_weight_half(name, w, h):
-            raw = keep.tile([P, PACK, 256], F32, name=f"{name}raw{h}", tag=f"wraw{h}")
-            nc.sync.dma_start(raw[:], w.rearrange("(p j) c -> p j c", j=PACK)[:, :, 256 * h : 256 * (h + 1)])
-            return raw
-
-        def deal(copy, grouped, raw, h, lo, hi):
-            copy(
-                grouped[:, :, 64 * h + lo : 64 * h + hi, :].rearrange("p t m j -> p m j t"),
-                raw[:, :, PACK * lo : PACK * hi].rearrange("p j (m t) -> p m j t", t=PACK),
-            )
 
         offs_t = load_list("offs", offs)
-        w1raw = [load_weight_half("w1", w1, 0)]
+        w1raw = keep.tile([P, PACK, H], F32, name="w1raw")
+        w1v = w1.rearrange("(p j) c -> p j c", j=PACK)
+        nc.sync.dma_start(w1raw[:], w1v)
         l1_t = load_list("l1", l1)
         r1_t = load_list("r1", r1)
-        xs = keep.tile([P, T], U8, name="xs", align_bytes=64)
+        xs = keep.tile([P, T], U8, name="xs", tag="xs", align_bytes=64)
         nc.vector.memset(xs[:].bitcast(I32), 0)
         for q in range(4):
             nc.sync.dma_start(xs[32 * q : 32 * q + 4, :].bitcast(I32), x_scales[0, 4 * q : 4 * q + 4, :].bitcast(I32))
-        xw = keep.tile([P, T], I32, name="xw", align_bytes=64)
+        xw = keep.tile([P, T], I32, name="xw", tag="xw", align_bytes=64)
         nc.sync.dma_start(xw[:], x_words[0].rearrange("p n t -> p (n t)").bitcast(I32))
-        w1raw.append(load_weight_half("w1", w1, 1))
+        f2 = load_share("f2", fr2)
+        f1 = load_share("f1", fr1)
         l2_t = load_list("l2", l2)
         r2_t = load_list("r2", r2)
-        f1 = load_share("f1", fr1)
-        f2 = load_share("f2", fr2)
+        w2raw = keep.tile([P, PACK, N], F32, name="w2raw")
+        nc.sync.dma_start(w2raw[:], w2.rearrange("(p j) c -> p j c", j=PACK))
 
         ident = keep.tile([P, P], F32, name="ident")
         make_identity(nc, ident[:])
 
         xq_s = keep.tile([P, S], U8, name="xq_s", align_bytes=64)
         nc.vector.tensor_copy(xq_s[:], xs[:].indirect(offs_t[:]))
-        xq_w = keep.tile([P, S], U32, name="xq_w", align_bytes=64)
-        nc.vector.tensor_copy(xq_w[:], xw[:].bitcast(U32).indirect(offs_t[:]))
-        w1g = keep.tile([P, PACK, P, PACK], BF16, name="w1g", align_bytes=64)
-        deal(nc.scalar.copy, w1g, w1raw[0], 0, 0, 64)
-        deal(nc.vector.tensor_copy, w1g, w1raw[1], 1, 0, 40)
-        deal(nc.scalar.copy, w1g, w1raw[1], 1, 40, 64)
 
-        ys = []
-        for t in range(PACK):
-            wc = keep.tile([P, P], U32, name=f"w1c{t}", align_bytes=64)
-            ws = keep.tile([P, P], U8, name=f"w1s{t}", align_bytes=64)
-            nc.vector.quantize_mx(wc[:].bitcast(FP8X4), ws[:], w1g[:, t].rearrange("p m j -> p (m j)"))
-            y = keep.tile([P, S], F32, name=f"y{t}")
-            if t == 0:
-                pieces = ((4, slice(0, 256), nc.scalar.copy), (0, slice(256, 512), nc.vector.tensor_copy))
-            else:
-                pieces = ((t, slice(0, S), nc.scalar.copy),)
-            for b, cols, copy in pieces:
-                acc = bank(b, f"yacc{t}_{b}")
-                nc.tensor.matmul_mx(acc[:, cols], wc[:].bitcast(FP8X4), ws[:], xq_w[:, cols].bitcast(FP8X4), xq_s[:, cols], start=True, stop=True)
-                copy(y[:, cols], acc[:, cols])
-            ys.append(y)
+        w1g = keep.tile([P, PACK, P, PACK], BF16, name="w1g", align_bytes=64)
+        for copy, lo, hi in ((nc.scalar.copy, 0, 80), (nc.vector.tensor_copy, 80, P)):
+            copy(
+                w1g[:, :, lo:hi, :].rearrange("p t m j -> p m j t"),
+                w1raw[:, :, PACK * lo : PACK * hi].rearrange("p j (m t) -> p m j t", t=PACK),
+            )
+        w1s = keep.tile([P, H], U8, name="w1s", align_bytes=64)
+        w1c0 = keep.tile([P, P], U32, name="w1c0", tag="xs", align_bytes=64)
+        nc.vector.quantize_mx(w1c0[:].bitcast(FP8X4), w1s[:, :P], w1g[:, 0].rearrange("p m j -> p (m j)"))
+
+        xq_w = []
+        for a in range(2):
+            xq = keep.tile([P, S // 2], U32, name=f"xq_w{a}", align_bytes=64)
+            nc.vector.tensor_copy(xq[:], xw[:].bitcast(U32).indirect(offs_t[:, 16 * a : 16 * (a + 1)]))
+            xq_w.append(xq)
+
+        w1c1 = keep.tile([P, 3 * P], U32, name="w1c1", tag="xw", align_bytes=64)
+        nc.vector.quantize_mx(w1c1[:, :P].bitcast(FP8X4), w1s[:, P : 2 * P], w1g[:, 1].rearrange("p m j -> p (m j)"))
+        nc.vector.quantize_mx(w1c1[:, P:].bitcast(FP8X4), w1s[:, 2 * P :], w1g[:, 2:4].rearrange("p t m j -> p (t m j)"))
+        w1c = [w1c0[:]] + [w1c1[:, P * t : P * (t + 1)] for t in range(3)]
 
         c1 = keep.tile([P, V], F32, name="c1")
-        nc.vector.tensor_scalar(c1[:], f1[:], -1.0, 1.0, ALU.mult, ALU.add)
         nf2 = keep.tile([P, V], F32, name="nf2")
-        nc.vector.tensor_scalar(nf2[:], f2[:], -1.0, None, ALU.mult)
         nc2 = keep.tile([P, V], F32, name="nc2")
-        nc.vector.tensor_scalar(nc2[:], f2[:], -1.0, None, ALU.add)
+        nc.scalar.activation(nf2[:], f2[:], ACT.Copy, bias=0.0, scale=-1.0)
+        nc.scalar.activation(nc2[:], f2[:], ACT.Copy, bias=-1.0, scale=1.0)
+        nc.scalar.activation(c1[:], f1[:], ACT.Copy, bias=1.0, scale=-1.0)
         terms = ((l1_t, f1), (r1_t, c1), (l2_t, nf2), (r2_t, nc2))
 
-        w2g = keep.tile([P, PACK, P, PACK], BF16, name="w2g", align_bytes=64)
-        w2raw = [load_weight_half("w2", w2, h) for h in range(2)]
-        w2c = keep.tile([P, N], U32, name="w2c", align_bytes=64)
-        w2s = keep.tile([P, N], U8, name="w2s", align_bytes=64)
+        def first_product(acc, t, lo, hi):
+            a, o = divmod(lo, S // 2)
+            rows = slice(P * t, P * (t + 1))
+            nc.tensor.matmul_mx(acc[:, lo:hi], w1c[t].bitcast(FP8X4), w1s[:, rows], xq_w[a][:, o : o + hi - lo].bitcast(FP8X4), xq_s[:, lo:hi], start=True, stop=True)
 
-        zacc = [bank(4, "zacc0"), bank(0, "zacc1")]
-        units = ((0, 0, 2), (1, 0, 2), (2, 0, 2), (3, 0, 1), (3, 1, 2))
+        ys = [keep.tile([P, S], F32, name=f"y{t}", tag=f"y{t}", align_bytes=64) for t in range(PACK)]
+        for b, lo, hi, copy in ((0, 0, 256, nc.scalar.copy), (1, 256, 384, nc.vector.tensor_copy), (2, 384, 512, nc.scalar.copy)):
+            acc = bank(b, f"yacc0_{b}")
+            first_product(acc, 0, lo, hi)
+            copy(ys[0][:, lo:hi], acc[:, lo:hi])
+        for t in range(1, PACK):
+            acc = bank(2 + t, f"yacc{t}")
+            first_product(acc, t, 0, 256)
+            first_product(acc, t, 256, 512)
+            nc.scalar.copy(ys[t][:], acc[:])
 
-        def gather(u, i):
-            t, h0, h1 = units[u]
+
+        w2g = keep.tile([P, N, PACK], BF16, name="w2g", align_bytes=64)
+
+        def cast_w2(lo, hi):
+            nc.scalar.copy(
+                w2g[:, lo:hi, :].rearrange("p (c i) j -> p c j i", i=PACK),
+                w2raw[:, :, lo:hi].rearrange("p j (c i) -> p c j i", i=PACK),
+            )
+
+        zacc = [bank(4, "zacc0"), bank(5, "zacc1")]
+        z = [keep.tile([P, P, PACK], BF16, name=f"z{h}", tag=f"z{h}", align_bytes=64) for h in range(2)]
+
+        def gather(t, i, h0, h1):
             lst, share = terms[i]
-            g = keep.tile([P, P * (h1 - h0)], F32, name=f"g{u}_{i}")
+            g = keep.tile([P, P * (h1 - h0)], F32, name=f"g{t}_{i}_{h0}")
             nc.vector.tensor_tensor(g[:], ys[t][:].indirect(lst[:, 8 * h0 : 8 * h1]), share[:, P * h0 : P * h1], ALU.mult)
-            return [g[:, P * b : P * (b + 1)] for b in range(h1 - h0)]
+            return g
 
         def turn(dst, src, start, stop):
             nc.tensor.matmul(dst, src, ident[:], start=start, stop=stop, is_transpose=True)
 
-        def turn_back(t, h0, first, rise):
-            for b in range(len(rise)):
-                dst = zacc[h0 + b][:, P * t : P * (t + 1)]
-                turn(dst, first[:, P * b : P * (b + 1)], True, False)
-                turn(dst, rise[b][:], False, True)
+        def blk(g, b):
+            return g[:, P * b : P * (b + 1)]
 
-        pending = None
-        for u, (t, h0, h1) in enumerate(units):
-            blocks = range(h1 - h0)
-            g1 = gather(u, 0)
-            g2 = gather(u, 1)
-            sacc = bank(5, f"sacc{u}")
-            for b in blocks:
-                turn(sacc[:, P * b : P * (b + 1)], g1[b], True, False)
-                turn(sacc[:, P * b : P * (b + 1)], g2[b], False, True)
-            first = keep.tile([P, P * len(blocks)], F32, name=f"first{u}")
-            nc.scalar.copy(first[:], sacc[:, : P * len(blocks)])
-            dacc = [bank((6, 2)[u % 2] + b, f"dacc{u}_{b}") for b in blocks]
-            for b in blocks:
-                turn(dacc[b][:, :P], g1[b], True, False)
-                turn(dacc[b][:, :P], g2[b], False, False)
-            if pending is not None:
-                turn_back(*pending)
-            n3 = gather(u, 2)
-            for b in blocks:
-                turn(dacc[b][:, :P], n3[b], False, False)
-            n4 = gather(u, 3)
+        def first_sample(t, dbanks):
+            g1 = gather(t, 0, 0, 2)
+            g2 = gather(t, 1, 0, 2)
+            sacc = bank(6 + t % 2, f"sacc{t}")
+            for h in range(2):
+                turn(blk(sacc, h), blk(g1, h), True, False)
+                turn(blk(sacc, h), blk(g2, h), False, True)
+            first = keep.tile([P, V], F32, name=f"first{t}")
+            nc.scalar.copy(first[:], sacc[:, :V])
+            dacc = [bank(b, f"dacc{t}_{b}") for b in dbanks]
+            for h, d in enumerate(dacc):
+                turn(d[:, :P], blk(g1, h), True, False)
+                turn(d[:, :P], blk(g2, h), False, False)
+            return first, dacc
+
+        def second_sample(t, dacc):
+            n3 = gather(t, 2, 0, len(dacc))
+            for h, d in enumerate(dacc):
+                turn(d[:, :P], blk(n3, h), False, False)
+            n4 = gather(t, 3, 0, len(dacc))
             rise = []
-            for b in blocks:
-                turn(dacc[b][:, :P], n4[b], False, True)
-                r = keep.tile([P, P], F32, name=f"rise{u}_{b}")
-                nc.scalar.activation(r[:], dacc[b][:, :P], ACT.Relu, scale=-1.0)
+            for h, d in enumerate(dacc):
+                turn(d[:, :P], blk(n4, h), False, True)
+                r = keep.tile([P, P], F32, name=f"rise{t}_{h}")
+                nc.scalar.activation(r[:], d[:, :P], ACT.Relu, scale=-1.0)
                 rise.append(r)
-            pending = (t, h0, first, rise)
-            if u < 2:
-                deal(nc.scalar.copy, w2g, w2raw[u], u, 0, 32)
-                deal(nc.scalar.copy, w2g, w2raw[u], u, 32, 64)
-        turn_back(*pending)
+            return rise
 
-        nc.vector.quantize_mx(w2c[:].bitcast(FP8X4), w2s[:], w2g[:].rearrange("p t m j -> p (t m j)"))
+        def turn_back(t, h, first, rise):
+            turn(blk(zacc[h], t), blk(first, h), True, False)
+            turn(blk(zacc[h], t), rise[h][:], False, True)
 
-        outv = out.rearrange("(p t) v -> p t v", t=PACK)
-        for h, zcopy in ((0, nc.vector.tensor_copy), (1, nc.scalar.copy)):
-            z = keep.tile([P, P, PACK], BF16, name=f"z{h}", align_bytes=64)
-            zcopy(z[:], zacc[h][:].rearrange("p (t v) -> p v t", t=PACK))
-            zc = keep.tile([P, P], U32, name=f"zc{h}", align_bytes=64)
+        first0, dacc0 = first_sample(0, (0, 1))
+        rise0 = second_sample(0, dacc0)
+        for k in range(0, 3):
+            cast_w2(64 * k, 64 * (k + 1))
+        first1, dacc1 = first_sample(1, (2, 3))
+        for h in range(2):
+            turn_back(0, h, first0, rise0)
+        rise1 = second_sample(1, dacc1)
+        for k in range(3, 6):
+            cast_w2(64 * k, 64 * (k + 1))
+        first2, dacc2 = first_sample(2, (0,))
+        for h in range(2):
+            turn_back(1, h, first1, rise1)
+        nc.scalar.copy(z[1][:, :, 0:2], zacc[1][:, : 2 * P].rearrange("p (t v) -> p v t", t=2))
+        for k in range(6, 8):
+            cast_w2(64 * k, 64 * (k + 1))
+        first3, dacc3 = first_sample(3, (1,))
+        turn(blk(zacc[1], 2), blk(first2, 1), True, True)
+        rise2 = second_sample(2, dacc2)
+        turn(blk(zacc[1], 3), blk(first3, 1), True, True)
+        rise3 = second_sample(3, dacc3)
+        turn_back(2, 0, first2, rise2)
+        turn_back(3, 0, first3, rise3)
+        nc.scalar.copy(z[0][:], zacc[0][:].rearrange("p (t v) -> p v t", t=PACK))
+
+        second = keep.tile([P, 2, P], F32, name="second")
+        n3 = gather(2, 2, 1, 2)
+        n4 = gather(2, 3, 1, 2)
+        m3 = gather(3, 2, 1, 2)
+        nc.vector.scalar_tensor_tensor(second[:, 0, :], n3[:], -1.0, n4[:], ALU.mult, ALU.subtract)
+        m4 = gather(3, 3, 1, 2)
+
+
+        w2c = keep.tile([P, N], U32, name="w2c", tag="y3", align_bytes=64)
+        w2s = keep.tile([P, N], U8, name="w2s", align_bytes=64)
+
+        def quantize_w2(lo, hi):
+            nc.vector.quantize_mx(w2c[:, lo:hi].bitcast(FP8X4), w2s[:, lo:hi], w2g[:, lo:hi, :].rearrange("p c j -> p (c j)"))
+
+        def quantize_z(h, tag):
+            zc = keep.tile([P, P], U32, name=f"zc{h}", tag=tag, align_bytes=64)
             zs = keep.tile([P, P], U8, name=f"zs{h}", align_bytes=64)
-            nc.vector.quantize_mx(zc[:].bitcast(FP8X4), zs[:], z[:].rearrange("p v t -> p (v t)"))
+            nc.vector.quantize_mx(zc[:].bitcast(FP8X4), zs[:], z[h][:].rearrange("p v t -> p (v t)"))
+            return zc, zs
+
+        zq = [quantize_z(0, "zc0")]
+        quantize_w2(0, 128)
+        nc.vector.scalar_tensor_tensor(second[:, 1, :], m3[:], -1.0, m4[:], ALU.mult, ALU.subtract)
+        quantize_w2(128, 384)
+        nc.vector.tensor_tensor(
+            z[1][:, :, 2:4],
+            zacc[1][:, 2 * P :].rearrange("p (t v) -> p v t", t=2),
+            second[:].rearrange("p t v -> p v t"),
+            ALU.max,
+        )
+        quantize_w2(384, 512)
+        zq.append(quantize_z(1, "z0"))
+
+
+        outv = out.rearrange("(t p) v -> p t v", t=PACK)
+        for h in range(2):
+            zc, zs = zq[h]
             res = keep.tile([P, PACK, P], F32, name=f"res{h}")
             if h == 0:
-                pieces = ((1, 0, 4, nc.scalar.copy, nc.sync),)
+                pieces = ((6, 0, 2, nc.scalar.copy, nc.sync), (2, 2, 4, nc.scalar.copy, nc.sync))
             else:
-                pieces = ((3, 0, 2, nc.scalar.copy, nc.scalar), (7, 2, 4, nc.vector.tensor_copy, nc.sync))
+                pieces = ((7, 0, 2, nc.scalar.copy, nc.scalar), (3, 2, 4, nc.vector.tensor_copy, nc.sync))
             for b, t0, t1, copy, queue in pieces:
                 acc = bank(b, f"oacc{h}_{b}")
                 for t in range(t0, t1):

@@ -122,6 +122,8 @@ def tile_picked_roial_none_p_kernel(tc, x_words, x_scales, w1, fr1, fr2, w2, off
 
         zacc = [bank(4, "zacc0"), bank(5, "zacc1")]
         z = [keep.tile([P, P, PACK], BF16, name=f"z{h}", tag=f"z{h}", align_bytes=64) for h in range(2)]
+        second = keep.tile([P, PACK, P], F32, name="second")
+        nc.gpsimd.memset(second[:, 0:2, :], -3.4028234663852886e38)
 
         def gather(t, i, h0, h1):
             lst, share = terms[i]
@@ -135,15 +137,15 @@ def tile_picked_roial_none_p_kernel(tc, x_words, x_scales, w1, fr1, fr2, w2, off
         def blk(g, b):
             return g[:, P * b : P * (b + 1)]
 
-        def first_sample(t, dbanks):
-            g1 = gather(t, 0, 0, 2)
-            g2 = gather(t, 1, 0, 2)
-            sacc = bank(6 + t % 2, f"sacc{t}")
-            for h in range(2):
+        def first_sample(t, h0, h1, sbank, dbanks):
+            g1 = gather(t, 0, h0, h1)
+            g2 = gather(t, 1, h0, h1)
+            sacc = bank(sbank, f"sacc{t}_{h0}")
+            for h in range(h1 - h0):
                 turn(blk(sacc, h), blk(g1, h), True, False)
                 turn(blk(sacc, h), blk(g2, h), False, True)
-            first = keep.tile([P, V], F32, name=f"first{t}")
-            nc.scalar.copy(first[:], sacc[:, :V])
+            first = keep.tile([P, P * (h1 - h0)], F32, name=f"first{t}_{h0}")
+            nc.scalar.copy(first[:], sacc[:, : P * (h1 - h0)])
             dacc = [bank(b, f"dacc{t}_{b}") for b in dbanks]
             for h, d in enumerate(dacc):
                 turn(d[:, :P], blk(g1, h), True, False)
@@ -167,63 +169,62 @@ def tile_picked_roial_none_p_kernel(tc, x_words, x_scales, w1, fr1, fr2, w2, off
             turn(blk(zacc[h], t), blk(first, h), True, False)
             turn(blk(zacc[h], t), rise[h][:], False, True)
 
-        first0, dacc0 = first_sample(0, (0, 1))
+        first0, dacc0 = first_sample(0, 0, 2, 6, (0, 1))
         rise0 = second_sample(0, dacc0)
-        for k in range(0, 3):
-            cast_w2(64 * k, 64 * (k + 1))
-        first1, dacc1 = first_sample(1, (2, 3))
+        cast_w2(0, 128)
+        cast_w2(128, 256)
+        first1, dacc1 = first_sample(1, 0, 2, 7, (2, 3))
         for h in range(2):
             turn_back(0, h, first0, rise0)
         rise1 = second_sample(1, dacc1)
-        for k in range(3, 6):
-            cast_w2(64 * k, 64 * (k + 1))
-        first2, dacc2 = first_sample(2, (0,))
+        first2, dacc2 = first_sample(2, 0, 1, 6, (0,))
         for h in range(2):
             turn_back(1, h, first1, rise1)
-        nc.scalar.copy(z[1][:, :, 0:2], zacc[1][:, : 2 * P].rearrange("p (t v) -> p v t", t=2))
-        for k in range(6, 8):
-            cast_w2(64 * k, 64 * (k + 1))
-        first3, dacc3 = first_sample(3, (1,))
-        turn(blk(zacc[1], 2), blk(first2, 1), True, True)
         rise2 = second_sample(2, dacc2)
-        turn(blk(zacc[1], 3), blk(first3, 1), True, True)
-        rise3 = second_sample(3, dacc3)
+        cast_w2(256, 384)
+        first3, dacc3 = first_sample(3, 0, 1, 7, (1,))
         turn_back(2, 0, first2, rise2)
+        rise3 = second_sample(3, dacc3)
+        last2, none2 = first_sample(2, 1, 2, 6, ())
         turn_back(3, 0, first3, rise3)
+        turn(blk(zacc[1], 2), last2[:], True, True)
         nc.scalar.copy(z[0][:], zacc[0][:].rearrange("p (t v) -> p v t", t=PACK))
+        last3, none3 = first_sample(3, 1, 2, 7, ())
+        turn(blk(zacc[1], 3), last3[:], True, True)
+        cast_w2(384, 512)
 
-        second = keep.tile([P, 2, P], F32, name="second")
         n3 = gather(2, 2, 1, 2)
         n4 = gather(2, 3, 1, 2)
         m3 = gather(3, 2, 1, 2)
-        nc.vector.scalar_tensor_tensor(second[:, 0, :], n3[:], -1.0, n4[:], ALU.mult, ALU.subtract)
         m4 = gather(3, 3, 1, 2)
 
 
         w2c = keep.tile([P, N], U32, name="w2c", tag="y3", align_bytes=64)
         w2s = keep.tile([P, N], U8, name="w2s", align_bytes=64)
+        zq = [(keep.tile([P, P], U32, name=f"zc{h}", tag=tag, align_bytes=64), keep.tile([P, P], U8, name=f"zs{h}", align_bytes=64)) for h, tag in enumerate(("zc0", "z0"))]
 
-        def quantize_w2(lo, hi):
-            nc.vector.quantize_mx(w2c[:, lo:hi].bitcast(FP8X4), w2s[:, lo:hi], w2g[:, lo:hi, :].rearrange("p c j -> p (c j)"))
+        def quantize_w2(cols):
+            nc.vector.quantize_mx(w2c[:, cols].bitcast(FP8X4), w2s[:, cols], w2g[:, cols, :].rearrange("p c j -> p (c j)"))
 
-        def quantize_z(h, tag):
-            zc = keep.tile([P, P], U32, name=f"zc{h}", tag=tag, align_bytes=64)
-            zs = keep.tile([P, P], U8, name=f"zs{h}", align_bytes=64)
-            nc.vector.quantize_mx(zc[:].bitcast(FP8X4), zs[:], z[h][:].rearrange("p v t -> p (v t)"))
-            return zc, zs
+        def quantize_z(h, cols):
+            zc, zs = zq[h]
+            nc.vector.quantize_mx(zc[:, cols].bitcast(FP8X4), zs[:, cols], z[h][:, cols, :].rearrange("p v t -> p (v t)"))
 
-        zq = [quantize_z(0, "zc0")]
-        quantize_w2(0, 128)
-        nc.vector.scalar_tensor_tensor(second[:, 1, :], m3[:], -1.0, m4[:], ALU.mult, ALU.subtract)
-        quantize_w2(128, 384)
-        nc.vector.tensor_tensor(
-            z[1][:, :, 2:4],
-            zacc[1][:, 2 * P :].rearrange("p (t v) -> p v t", t=2),
-            second[:].rearrange("p t v -> p v t"),
-            ALU.max,
-        )
-        quantize_w2(384, 512)
-        zq.append(quantize_z(1, "z0"))
+        nc.vector.scalar_tensor_tensor(second[:, 2, :], n3[:], -1.0, n4[:], ALU.mult, ALU.subtract)
+        quantize_w2(slice(0, 256))
+        nc.vector.scalar_tensor_tensor(second[:, 3, :], m3[:], -1.0, m4[:], ALU.mult, ALU.subtract)
+        quantize_z(0, slice(0, P))
+        quantize_w2(slice(256, 512))
+        parts = (slice(0, 64), slice(64, P))
+        for cols in parts:
+            nc.vector.tensor_tensor(
+                z[1][:, cols, :].rearrange("p (c i) t -> p c t i", i=PACK),
+                zacc[1][:].rearrange("p (t v) -> p t v", t=PACK)[:, :, cols].rearrange("p t (c i) -> p c t i", i=PACK),
+                second[:, :, cols].rearrange("p t (c i) -> p c t i", i=PACK),
+                ALU.max,
+            )
+        for cols in parts:
+            quantize_z(1, cols)
 
 
         outv = out.rearrange("(t p) v -> p t v", t=PACK)

@@ -116,8 +116,8 @@ def tile_picked_roial_none_p_kernel(tc, x_words, x_scales, w1, fr1, fr2, w2, off
 
         def cast_w2(lo, hi):
             nc.scalar.copy(
-                w2g[:, lo:hi, :].rearrange("p (c i) j -> p c j i", i=PACK),
-                w2raw[:, :, lo:hi].rearrange("p j (c i) -> p c j i", i=PACK),
+                w2g[:, lo:hi, :],
+                w2raw[:, :, lo:hi].rearrange("p j c -> p c j"),
             )
 
         zacc = [bank(4, "zacc0"), bank(5, "zacc1")]
@@ -218,9 +218,9 @@ def tile_picked_roial_none_p_kernel(tc, x_words, x_scales, w1, fr1, fr2, w2, off
         parts = (slice(0, 64), slice(64, P))
         for cols in parts:
             nc.vector.tensor_tensor(
-                z[1][:, cols, :].rearrange("p (c i) t -> p c t i", i=PACK),
-                zacc[1][:].rearrange("p (t v) -> p t v", t=PACK)[:, :, cols].rearrange("p t (c i) -> p c t i", i=PACK),
-                second[:, :, cols].rearrange("p t (c i) -> p c t i", i=PACK),
+                z[1][:, cols, :],
+                zacc[1][:].rearrange("p (t v) -> p v t", t=PACK)[:, cols, :],
+                second[:, :, cols].rearrange("p t v -> p v t"),
                 ALU.max,
             )
         for cols in parts:

@@ -234,7 +234,7 @@ def tile_picked_roial_none_p_kernel(tc, x_words, x_scales, w1, fr1, fr2, w2, off
             if h == 0:
                 pieces = ((6, 0, 2, nc.scalar.copy, nc.sync), (2, 2, 4, nc.scalar.copy, nc.sync))
             else:
-                pieces = ((7, 0, 2, nc.scalar.copy, nc.scalar), (3, 2, 4, nc.vector.tensor_copy, nc.sync))
+                pieces = ((7, 0, 2, nc.scalar.copy, nc.sync), (3, 2, 4, nc.vector.tensor_copy, nc.sync))
             for b, t0, t1, copy, queue in pieces:
                 acc = bank(b, f"oacc{h}_{b}")
                 for t in range(t0, t1):

@@ -49,8 +49,8 @@ def tile_picked_roial_none_p_kernel(tc, x_words, x_scales, w1, fr1, fr2, w2, off
         r1_t = load_list("r1", r1)
         xs = keep.tile([P, T], U8, name="xs", tag="xs", align_bytes=64)
         nc.vector.memset(xs[:].bitcast(I32), 0)
-        for q in range(4):
-            nc.sync.dma_start(xs[32 * q : 32 * q + 4, :].bitcast(I32), x_scales[0, 4 * q : 4 * q + 4, :].bitcast(I32))
+        for r in range(4):
+            nc.sync.dma_start(xs[r:P:32, :].bitcast(I32), x_scales[0, r:16:4, :].bitcast(I32))
         xw = keep.tile([P, T], I32, name="xw", tag="xw", align_bytes=64)
         nc.sync.dma_start(xw[:], x_words[0].rearrange("p n t -> p (n t)").bitcast(I32))
         f2 = load_share("f2", fr2)

@@ -73,8 +73,8 @@ def tile_picked_roial_none_p_kernel(tc, x_words, x_scales, w1, fr1, fr2, w2, off
                 w1raw[:, :, PACK * lo : PACK * hi].rearrange("p j (m t) -> p m j t", t=PACK),
             )
         w1s = keep.tile([P, H], U8, name="w1s", align_bytes=64)
-        w1c0 = keep.tile([P, P], U32, name="w1c0", tag="xs", align_bytes=64)
-        nc.vector.quantize_mx(w1c0[:].bitcast(FP8X4), w1s[:, :P], w1g[:, 0].rearrange("p m j -> p (m j)"))
+        w1c0 = keep.tile([P, 2 * P], U32, name="w1c0", tag="xs", align_bytes=64)
+        nc.vector.quantize_mx(w1c0[:].bitcast(FP8X4), w1s[:, : 2 * P], w1g[:, 0:2].rearrange("p t m j -> p (t m j)"))
 
         xq_w = []
         for a in range(2):
@@ -82,10 +82,9 @@ def tile_picked_roial_none_p_kernel(tc, x_words, x_scales, w1, fr1, fr2, w2, off
             nc.vector.tensor_copy(xq[:], xw[:].bitcast(U32).indirect(offs_t[:, 16 * a : 16 * (a + 1)]))
             xq_w.append(xq)
 
-        w1c1 = keep.tile([P, 3 * P], U32, name="w1c1", tag="xw", align_bytes=64)
-        nc.vector.quantize_mx(w1c1[:, :P].bitcast(FP8X4), w1s[:, P : 2 * P], w1g[:, 1].rearrange("p m j -> p (m j)"))
-        nc.vector.quantize_mx(w1c1[:, P:].bitcast(FP8X4), w1s[:, 2 * P :], w1g[:, 2:4].rearrange("p t m j -> p (t m j)"))
-        w1c = [w1c0[:]] + [w1c1[:, P * t : P * (t + 1)] for t in range(3)]
+        w1c1 = keep.tile([P, 2 * P], U32, name="w1c1", tag="xw", align_bytes=64)
+        nc.vector.quantize_mx(w1c1[:].bitcast(FP8X4), w1s[:, 2 * P :], w1g[:, 2:4].rearrange("p t m j -> p (t m j)"))
+        w1c = [c[:, P * t : P * (t + 1)] for c in (w1c0, w1c1) for t in range(2)]
 
         c1 = keep.tile([P, V], F32, name="c1")
         nf2 = keep.tile([P, V], F32, name="nf2")
@@ -176,12 +175,13 @@ def tile_picked_roial_none_p_kernel(tc, x_words, x_scales, w1, fr1, fr2, w2, off
         first1, dacc1 = first_sample(1, 0, 2, 7, (2, 3))
         for h in range(2):
             turn_back(0, h, first0, rise0)
+        cast_w2(256, 384)
         rise1 = second_sample(1, dacc1)
+        cast_w2(384, 512)
         first2, dacc2 = first_sample(2, 0, 1, 6, (0,))
         for h in range(2):
             turn_back(1, h, first1, rise1)
         rise2 = second_sample(2, dacc2)
-        cast_w2(256, 384)
         first3, dacc3 = first_sample(3, 0, 1, 7, (1,))
         turn_back(2, 0, first2, rise2)
         rise3 = second_sample(3, dacc3)
@@ -191,7 +191,6 @@ def tile_picked_roial_none_p_kernel(tc, x_words, x_scales, w1, fr1, fr2, w2, off
         nc.scalar.copy(z[0][:], zacc[0][:].rearrange("p (t v) -> p v t", t=PACK))
         last3, none3 = first_sample(3, 1, 2, 7, ())
         turn(blk(zacc[1], 3), last3[:], True, True)
-        cast_w2(384, 512)
 
         n3 = gather(2, 2, 1, 2)
         n4 = gather(2, 3, 1, 2)
@@ -211,10 +210,9 @@ def tile_picked_roial_none_p_kernel(tc, x_words, x_scales, w1, fr1, fr2, w2, off
             nc.vector.quantize_mx(zc[:, cols].bitcast(FP8X4), zs[:, cols], z[h][:, cols, :].rearrange("p v t -> p (v t)"))
 
         nc.vector.scalar_tensor_tensor(second[:, 2, :], n3[:], -1.0, n4[:], ALU.mult, ALU.subtract)
-        quantize_w2(slice(0, 256))
+        quantize_w2(slice(0, 512))
         nc.vector.scalar_tensor_tensor(second[:, 3, :], m3[:], -1.0, m4[:], ALU.mult, ALU.subtract)
         quantize_z(0, slice(0, P))
-        quantize_w2(slice(256, 512))
         parts = (slice(0, 64), slice(64, P))
         for cols in parts:
             nc.vector.tensor_tensor(
@@ -241,4 +239,7 @@ def tile_picked_roial_none_p_kernel(tc, x_words, x_scales, w1, fr1, fr2, w2, off
                     cols = slice(P * t, P * (t + 1))
                     nc.tensor.matmul_mx(acc[:, cols], w2c[:, cols].bitcast(FP8X4), w2s[:, cols], zc[:].bitcast(FP8X4), zs[:], start=True, stop=True)
                 copy(res[:, t0:t1, :], acc[:, P * t0 : P * t1].rearrange("p (t v) -> p t v", v=P))
-                queue.dma_start(outv[:, t0:t1, P * h : P * (h + 1)], res[:, t0:t1, :])
+                if h == 1:
+                    queue.dma_start(outv[:, t0:t1, P:], res[:, t0:t1, :])
+            if h == 0:
+                nc.sync.dma_start(outv[:, :, :P], res[:])

@@ -19,6 +19,7 @@ ACT = mybir.ActivationFunctionType
 P = 128
 PACK = 4
 BANK = 512
+LOWEST = -3.4028234663852886e38
 
 
 def tile_picked_roial_none_p_kernel(tc, x_words, x_scales, w1, fr1, fr2, w2, offs, l1, r1, l2, r2, out):
@@ -40,76 +41,73 @@ def tile_picked_roial_none_p_kernel(tc, x_words, x_scales, w1, fr1, fr2, w2, off
             nc.sync.dma_start(f[:], src.rearrange("(p j) v -> p j v", j=PACK)[:, 0, :])
             return f
 
-
         offs_t = load_list("offs", offs)
-        w1raw = keep.tile([P, PACK, H], F32, name="w1raw")
-        w1v = w1.rearrange("(p j) c -> p j c", j=PACK)
-        nc.sync.dma_start(w1raw[:], w1v)
+        xw = keep.tile([P, T], I32, name="xw", align_bytes=64)
+        nc.sync.dma_start(xw[:], x_words[0].rearrange("p n t -> p (n t)").bitcast(I32))
         l1_t = load_list("l1", l1)
         r1_t = load_list("r1", r1)
-        xs = keep.tile([P, T], U8, name="xs", tag="xs", align_bytes=64)
+        xs = keep.tile([P, T], U8, name="xs", align_bytes=64)
         nc.vector.memset(xs[:].bitcast(I32), 0)
         for r in range(4):
             nc.sync.dma_start(xs[r:P:32, :].bitcast(I32), x_scales[0, r:16:4, :].bitcast(I32))
-        xw = keep.tile([P, T], I32, name="xw", tag="xw", align_bytes=64)
-        nc.sync.dma_start(xw[:], x_words[0].rearrange("p n t -> p (n t)").bitcast(I32))
-        f2 = load_share("f2", fr2)
+        w1raw = keep.tile([P, PACK, H], F32, name="w1raw")
+        nc.sync.dma_start(w1raw[:], w1.rearrange("(p j) c -> p j c", j=PACK))
         f1 = load_share("f1", fr1)
+        f2 = load_share("f2", fr2)
         l2_t = load_list("l2", l2)
         r2_t = load_list("r2", r2)
         w2raw = keep.tile([P, PACK, N], F32, name="w2raw")
-        nc.sync.dma_start(w2raw[:], w2.rearrange("(p j) c -> p j c", j=PACK))
+        w2rows = w2.rearrange("(q t i) c -> t q i c", t=PACK, i=4)
+        for t in range(PACK):
+            nc.sync.dma_start(w2raw[:, t, :], w2rows[t])
 
         ident = keep.tile([P, P], F32, name="ident")
         make_identity(nc, ident[:])
+        second = keep.tile([P, PACK, P], F32, name="second")
+        nc.scalar.activation(second[:, 0:2, :], ident[:].unsqueeze(1).to_broadcast([P, 2, P]), ACT.Copy, bias=LOWEST, scale=0.0)
 
+        xq_w = keep.tile([P, S], U32, name="xq_w", align_bytes=64)
+        nc.vector.tensor_copy(xq_w[:], xw[:].bitcast(U32).indirect(offs_t[:]))
         xq_s = keep.tile([P, S], U8, name="xq_s", align_bytes=64)
         nc.vector.tensor_copy(xq_s[:], xs[:].indirect(offs_t[:]))
 
-        w1g = keep.tile([P, PACK, P, PACK], BF16, name="w1g", align_bytes=64)
-        for copy, lo, hi in ((nc.scalar.copy, 0, 80), (nc.vector.tensor_copy, 80, P)):
-            copy(
-                w1g[:, :, lo:hi, :].rearrange("p t m j -> p m j t"),
-                w1raw[:, :, PACK * lo : PACK * hi].rearrange("p j (m t) -> p m j t", t=PACK),
-            )
+        w1cols = w1raw[:].rearrange("p j (q t i) -> p t q j i", t=PACK, i=4)
+        w1g = [keep.tile([P, P, PACK], BF16, name=f"w1g{t}", align_bytes=64) for t in range(2)]
+        w1late = keep.tile([P, 2, P, PACK], BF16, name="w1late", align_bytes=64)
+        nc.vector.tensor_copy(w1g[0][:].rearrange("p (q i) j -> p q j i", i=4)[:, :24], w1cols[:, 0, :24])
+        nc.scalar.copy(w1g[0][:].rearrange("p (q i) j -> p q j i", i=4)[:, 24:], w1cols[:, 0, 24:])
+        nc.vector.tensor_copy(w1g[1][:].rearrange("p (q i) j -> p q j i", i=4), w1cols[:, 1])
+        for t in range(2):
+            nc.scalar.copy(w1late[:, t].rearrange("p (q i) j -> p q j i", i=4), w1cols[:, 2 + t])
+        w1c = keep.tile([P, H], U32, name="w1c", align_bytes=64)
         w1s = keep.tile([P, H], U8, name="w1s", align_bytes=64)
-        w1c0 = keep.tile([P, 2 * P], U32, name="w1c0", tag="xs", align_bytes=64)
-        nc.vector.quantize_mx(w1c0[:].bitcast(FP8X4), w1s[:, : 2 * P], w1g[:, 0:2].rearrange("p t m j -> p (t m j)"))
-
-        xq_w = []
-        for a in range(2):
-            xq = keep.tile([P, S // 2], U32, name=f"xq_w{a}", align_bytes=64)
-            nc.vector.tensor_copy(xq[:], xw[:].bitcast(U32).indirect(offs_t[:, 16 * a : 16 * (a + 1)]))
-            xq_w.append(xq)
-
-        w1c1 = keep.tile([P, 2 * P], U32, name="w1c1", tag="xw", align_bytes=64)
-        nc.vector.quantize_mx(w1c1[:].bitcast(FP8X4), w1s[:, 2 * P :], w1g[:, 2:4].rearrange("p t m j -> p (t m j)"))
-        w1c = [c[:, P * t : P * (t + 1)] for c in (w1c0, w1c1) for t in range(2)]
+        for t in range(2):
+            cols = slice(P * t, P * (t + 1))
+            nc.vector.quantize_mx(w1c[:, cols].bitcast(FP8X4), w1s[:, cols], w1g[t][:].rearrange("p m j -> p (m j)"))
 
         c1 = keep.tile([P, V], F32, name="c1")
-        nf2 = keep.tile([P, V], F32, name="nf2")
+        nf2 = keep.tile([P, V], F32, name="nf2", tag="nf2", align_bytes=64)
         nc2 = keep.tile([P, V], F32, name="nc2")
-        nc.scalar.activation(nf2[:], f2[:], ACT.Copy, bias=0.0, scale=-1.0)
-        nc.scalar.activation(nc2[:], f2[:], ACT.Copy, bias=-1.0, scale=1.0)
-        nc.scalar.activation(c1[:], f1[:], ACT.Copy, bias=1.0, scale=-1.0)
+        nc.vector.tensor_scalar(c1[:], f1[:], -1.0, 1.0, ALU.mult, ALU.add)
+        nc.vector.tensor_scalar(nf2[:], f2[:], -1.0, 0.0, ALU.mult, ALU.add)
+        nc.vector.tensor_scalar(nc2[:], f2[:], 1.0, -1.0, ALU.mult, ALU.add)
         terms = ((l1_t, f1), (r1_t, c1), (l2_t, nf2), (r2_t, nc2))
 
         def first_product(acc, t, lo, hi):
-            a, o = divmod(lo, S // 2)
             rows = slice(P * t, P * (t + 1))
-            nc.tensor.matmul_mx(acc[:, lo:hi], w1c[t].bitcast(FP8X4), w1s[:, rows], xq_w[a][:, o : o + hi - lo].bitcast(FP8X4), xq_s[:, lo:hi], start=True, stop=True)
+            nc.tensor.matmul_mx(acc[:, lo:hi], w1c[:, rows].bitcast(FP8X4), w1s[:, rows], xq_w[:, lo:hi].bitcast(FP8X4), xq_s[:, lo:hi], start=True, stop=True)
 
         ys = [keep.tile([P, S], F32, name=f"y{t}", tag=f"y{t}", align_bytes=64) for t in range(PACK)]
-        for b, lo, hi, copy in ((0, 0, 256, nc.scalar.copy), (1, 256, 384, nc.vector.tensor_copy), (2, 384, 512, nc.scalar.copy)):
+        for b, lo, hi, copy in ((0, 0, 256, nc.vector.tensor_copy), (1, 256, 384, nc.scalar.copy), (2, 384, 512, nc.scalar.copy)):
             acc = bank(b, f"yacc0_{b}")
             first_product(acc, 0, lo, hi)
             copy(ys[0][:, lo:hi], acc[:, lo:hi])
+        nc.vector.quantize_mx(w1c[:, 2 * P :].bitcast(FP8X4), w1s[:, 2 * P :], w1late[:].rearrange("p t m j -> p (t m j)"))
         for t in range(1, PACK):
             acc = bank(2 + t, f"yacc{t}")
             first_product(acc, t, 0, 256)
             first_product(acc, t, 256, 512)
             nc.scalar.copy(ys[t][:], acc[:])
-
 
         w2g = keep.tile([P, N, PACK], BF16, name="w2g", align_bytes=64)
 
@@ -121,8 +119,6 @@ def tile_picked_roial_none_p_kernel(tc, x_words, x_scales, w1, fr1, fr2, w2, off
 
         zacc = [bank(4, "zacc0"), bank(5, "zacc1")]
         z = [keep.tile([P, P, PACK], BF16, name=f"z{h}", tag=f"z{h}", align_bytes=64) for h in range(2)]
-        second = keep.tile([P, PACK, P], F32, name="second")
-        nc.gpsimd.memset(second[:, 0:2, :], -3.4028234663852886e38)
 
         def gather(t, i, h0, h1):
             lst, share = terms[i]
@@ -188,8 +184,10 @@ def tile_picked_roial_none_p_kernel(tc, x_words, x_scales, w1, fr1, fr2, w2, off
         last2, none2 = first_sample(2, 1, 2, 6, ())
         turn_back(3, 0, first3, rise3)
         turn(blk(zacc[1], 2), last2[:], True, True)
-        nc.scalar.copy(z[0][:], zacc[0][:].rearrange("p (t v) -> p v t", t=PACK))
+        z0_sums = zacc[0][:].rearrange("p (t v) -> p v t", t=PACK)
+        nc.scalar.copy(z[0][:, :64], z0_sums[:, :64])
         last3, none3 = first_sample(3, 1, 2, 7, ())
+        nc.scalar.copy(z[0][:, 64:], z0_sums[:, 64:])
         turn(blk(zacc[1], 3), last3[:], True, True)
 
         n3 = gather(2, 2, 1, 2)
@@ -210,9 +208,10 @@ def tile_picked_roial_none_p_kernel(tc, x_words, x_scales, w1, fr1, fr2, w2, off
             nc.vector.quantize_mx(zc[:, cols].bitcast(FP8X4), zs[:, cols], z[h][:, cols, :].rearrange("p v t -> p (v t)"))
 
         nc.vector.scalar_tensor_tensor(second[:, 2, :], n3[:], -1.0, n4[:], ALU.mult, ALU.subtract)
-        quantize_w2(slice(0, 512))
+        quantize_w2(slice(0, 256))
         nc.vector.scalar_tensor_tensor(second[:, 3, :], m3[:], -1.0, m4[:], ALU.mult, ALU.subtract)
         quantize_z(0, slice(0, P))
+        quantize_w2(slice(256, 512))
         parts = (slice(0, 64), slice(64, P))
         for cols in parts:
             nc.vector.tensor_tensor(
@@ -239,7 +238,4 @@ def tile_picked_roial_none_p_kernel(tc, x_words, x_scales, w1, fr1, fr2, w2, off
                     cols = slice(P * t, P * (t + 1))
                     nc.tensor.matmul_mx(acc[:, cols], w2c[:, cols].bitcast(FP8X4), w2s[:, cols], zc[:].bitcast(FP8X4), zs[:], start=True, stop=True)
                 copy(res[:, t0:t1, :], acc[:, P * t0 : P * t1].rearrange("p (t v) -> p t v", v=P))
-                if h == 1:
-                    queue.dma_start(outv[:, t0:t1, P:], res[:, t0:t1, :])
-            if h == 0:
-                nc.sync.dma_start(outv[:, :, :P], res[:])
+                queue.dma_start(outv[:, t0:t1, P * h : P * (h + 1)], res[:, t0:t1, :])

@@ -19,7 +19,6 @@ ACT = mybir.ActivationFunctionType
 P = 128
 PACK = 4
 BANK = 512
-LOWEST = -3.4028234663852886e38
 
 
 def tile_picked_roial_none_p_kernel(tc, x_words, x_scales, w1, fr1, fr2, w2, offs, l1, r1, l2, r2, out):
@@ -63,8 +62,6 @@ def tile_picked_roial_none_p_kernel(tc, x_words, x_scales, w1, fr1, fr2, w2, off
 
         ident = keep.tile([P, P], F32, name="ident")
         make_identity(nc, ident[:])
-        second = keep.tile([P, PACK, P], F32, name="second")
-        nc.scalar.activation(second[:, 0:2, :], ident[:].unsqueeze(1).to_broadcast([P, 2, P]), ACT.Copy, bias=LOWEST, scale=0.0)
 
         xq_w = keep.tile([P, S], U32, name="xq_w", align_bytes=64)
         nc.vector.tensor_copy(xq_w[:], xw[:].bitcast(U32).indirect(offs_t[:]))
@@ -72,59 +69,38 @@ def tile_picked_roial_none_p_kernel(tc, x_words, x_scales, w1, fr1, fr2, w2, off
         nc.vector.tensor_copy(xq_s[:], xs[:].indirect(offs_t[:]))
 
         w1cols = w1raw[:].rearrange("p j (q t i) -> p t q j i", t=PACK, i=4)
-        w1g = [keep.tile([P, P, PACK], BF16, name=f"w1g{t}", align_bytes=64) for t in range(2)]
-        w1late = keep.tile([P, 2, P, PACK], BF16, name="w1late", align_bytes=64)
-        nc.vector.tensor_copy(w1g[0][:].rearrange("p (q i) j -> p q j i", i=4)[:, :24], w1cols[:, 0, :24])
-        nc.scalar.copy(w1g[0][:].rearrange("p (q i) j -> p q j i", i=4)[:, 24:], w1cols[:, 0, 24:])
-        nc.vector.tensor_copy(w1g[1][:].rearrange("p (q i) j -> p q j i", i=4), w1cols[:, 1])
+        w1g = [keep.tile([P, P, PACK], BF16, name=f"w1g{t}", align_bytes=64) for t in range(PACK)]
         for t in range(2):
-            nc.scalar.copy(w1late[:, t].rearrange("p (q i) j -> p q j i", i=4), w1cols[:, 2 + t])
-        w1c = keep.tile([P, H], U32, name="w1c", align_bytes=64)
-        w1s = keep.tile([P, H], U8, name="w1s", align_bytes=64)
-        for t in range(2):
-            cols = slice(P * t, P * (t + 1))
-            nc.vector.quantize_mx(w1c[:, cols].bitcast(FP8X4), w1s[:, cols], w1g[t][:].rearrange("p m j -> p (m j)"))
+            nc.vector.tensor_copy(w1g[t][:].rearrange("p (q i) j -> p q j i", i=4), w1cols[:, t])
+        for t in range(2, PACK):
+            nc.scalar.copy(w1g[t][:].rearrange("p (q i) j -> p q j i", i=4), w1cols[:, t])
+        w1c = [keep.tile([P, P], U32, name=f"w1c{t}", align_bytes=64) for t in range(PACK)]
+        w1s = [keep.tile([P, P], U8, name=f"w1s{t}", align_bytes=64) for t in range(PACK)]
+
+        def quantize_w1(t):
+            nc.vector.quantize_mx(w1c[t][:].bitcast(FP8X4), w1s[t][:], w1g[t][:].rearrange("p m j -> p (m j)"))
+
+        for t in range(3):
+            quantize_w1(t)
 
         c1 = keep.tile([P, V], F32, name="c1")
-        nf2 = keep.tile([P, V], F32, name="nf2", tag="nf2", align_bytes=64)
-        nc2 = keep.tile([P, V], F32, name="nc2")
         nc.vector.tensor_scalar(c1[:], f1[:], -1.0, 1.0, ALU.mult, ALU.add)
-        nc.vector.tensor_scalar(nf2[:], f2[:], -1.0, 0.0, ALU.mult, ALU.add)
-        nc.vector.tensor_scalar(nc2[:], f2[:], 1.0, -1.0, ALU.mult, ALU.add)
-        terms = ((l1_t, f1), (r1_t, c1), (l2_t, nf2), (r2_t, nc2))
 
         def first_product(acc, t, lo, hi):
-            rows = slice(P * t, P * (t + 1))
-            nc.tensor.matmul_mx(acc[:, lo:hi], w1c[:, rows].bitcast(FP8X4), w1s[:, rows], xq_w[:, lo:hi].bitcast(FP8X4), xq_s[:, lo:hi], start=True, stop=True)
+            nc.tensor.matmul_mx(acc[:, lo:hi], w1c[t][:].bitcast(FP8X4), w1s[t][:], xq_w[:, lo:hi].bitcast(FP8X4), xq_s[:, lo:hi], start=True, stop=True)
 
         ys = [keep.tile([P, S], F32, name=f"y{t}", tag=f"y{t}", align_bytes=64) for t in range(PACK)]
         for b, lo, hi, copy in ((0, 0, 256, nc.vector.tensor_copy), (1, 256, 384, nc.scalar.copy), (2, 384, 512, nc.scalar.copy)):
             acc = bank(b, f"yacc0_{b}")
             first_product(acc, 0, lo, hi)
             copy(ys[0][:, lo:hi], acc[:, lo:hi])
-        nc.vector.quantize_mx(w1c[:, 2 * P :].bitcast(FP8X4), w1s[:, 2 * P :], w1late[:].rearrange("p t m j -> p (t m j)"))
+        quantize_w1(3)
+        yacc = [None]
         for t in range(1, PACK):
             acc = bank(2 + t, f"yacc{t}")
             first_product(acc, t, 0, 256)
             first_product(acc, t, 256, 512)
-            nc.scalar.copy(ys[t][:], acc[:])
-
-        w2g = keep.tile([P, N, PACK], BF16, name="w2g", align_bytes=64)
-
-        def cast_w2(lo, hi):
-            nc.scalar.copy(
-                w2g[:, lo:hi, :],
-                w2raw[:, :, lo:hi].rearrange("p j c -> p c j"),
-            )
-
-        zacc = [bank(4, "zacc0"), bank(5, "zacc1")]
-        z = [keep.tile([P, P, PACK], BF16, name=f"z{h}", tag=f"z{h}", align_bytes=64) for h in range(2)]
-
-        def gather(t, i, h0, h1):
-            lst, share = terms[i]
-            g = keep.tile([P, P * (h1 - h0)], F32, name=f"g{t}_{i}_{h0}")
-            nc.vector.tensor_tensor(g[:], ys[t][:].indirect(lst[:, 8 * h0 : 8 * h1]), share[:, P * h0 : P * h1], ALU.mult)
-            return g
+            yacc.append(acc)
 
         def turn(dst, src, start, stop):
             nc.tensor.matmul(dst, src, ident[:], start=start, stop=stop, is_transpose=True)
@@ -132,110 +108,130 @@ def tile_picked_roial_none_p_kernel(tc, x_words, x_scales, w1, fr1, fr2, w2, off
         def blk(g, b):
             return g[:, P * b : P * (b + 1)]
 
-        def first_sample(t, h0, h1, sbank, dbanks):
-            g1 = gather(t, 0, h0, h1)
-            g2 = gather(t, 1, h0, h1)
-            sacc = bank(sbank, f"sacc{t}_{h0}")
-            for h in range(h1 - h0):
-                turn(blk(sacc, h), blk(g1, h), True, False)
-                turn(blk(sacc, h), blk(g2, h), False, True)
-            first = keep.tile([P, P * (h1 - h0)], F32, name=f"first{t}_{h0}")
-            nc.scalar.copy(first[:], sacc[:, : P * (h1 - h0)])
-            dacc = [bank(b, f"dacc{t}_{b}") for b in dbanks]
-            for h, d in enumerate(dacc):
-                turn(d[:, :P], blk(g1, h), True, False)
-                turn(d[:, :P], blk(g2, h), False, False)
-            return first, dacc
+        def buf(name, width, dtype=F32, tag=None):
+            return keep.tile([P, width], dtype, name=name, tag=tag or name, align_bytes=64)
 
-        def second_sample(t, dacc):
-            n3 = gather(t, 2, 0, len(dacc))
-            for h, d in enumerate(dacc):
-                turn(d[:, :P], blk(n3, h), False, False)
-            n4 = gather(t, 3, 0, len(dacc))
-            rise = []
-            for h, d in enumerate(dacc):
-                turn(d[:, :P], blk(n4, h), False, True)
-                r = keep.tile([P, P], F32, name=f"rise{t}_{h}")
-                nc.scalar.activation(r[:], d[:, :P], ACT.Relu, scale=-1.0)
-                rise.append(r)
-            return rise
-
-        def turn_back(t, h, first, rise):
-            turn(blk(zacc[h], t), blk(first, h), True, False)
-            turn(blk(zacc[h], t), rise[h][:], False, True)
-
-        first0, dacc0 = first_sample(0, 0, 2, 6, (0, 1))
-        rise0 = second_sample(0, dacc0)
-        cast_w2(0, 128)
-        cast_w2(128, 256)
-        first1, dacc1 = first_sample(1, 0, 2, 7, (2, 3))
+        f2acc = bank(1, "f2acc")
         for h in range(2):
-            turn_back(0, h, first0, rise0)
-        cast_w2(256, 384)
-        rise1 = second_sample(1, dacc1)
-        cast_w2(384, 512)
-        first2, dacc2 = first_sample(2, 0, 1, 6, (0,))
-        for h in range(2):
-            turn_back(1, h, first1, rise1)
-        rise2 = second_sample(2, dacc2)
-        first3, dacc3 = first_sample(3, 0, 1, 7, (1,))
-        turn_back(2, 0, first2, rise2)
-        rise3 = second_sample(3, dacc3)
-        last2, none2 = first_sample(2, 1, 2, 6, ())
-        turn_back(3, 0, first3, rise3)
-        turn(blk(zacc[1], 2), last2[:], True, True)
-        z0_sums = zacc[0][:].rearrange("p (t v) -> p v t", t=PACK)
-        nc.scalar.copy(z[0][:, :64], z0_sums[:, :64])
-        last3, none3 = first_sample(3, 1, 2, 7, ())
-        nc.scalar.copy(z[0][:, 64:], z0_sums[:, 64:])
-        turn(blk(zacc[1], 3), last3[:], True, True)
+            turn(blk(f2acc, h), blk(f2, h), True, True)
+        f2t = keep.tile([P, 16], F32, name="f2t")
 
-        n3 = gather(2, 2, 1, 2)
-        n4 = gather(2, 3, 1, 2)
-        m3 = gather(3, 2, 1, 2)
-        m4 = gather(3, 3, 1, 2)
+        nq = keep.tile([P, PACK, V], F32, name="nq")
+        zacc = [bank(3, "zacc0"), bank(4, "zacc1")]
+        z = [keep.tile([P, P, PACK], BF16, name=f"z{h}", tag=f"z{h}", align_bytes=64) for h in range(2)]
+        fars = []
 
+        def fetch_near(t, tag):
+            near = buf(f"near{t}", 2 * V, tag=tag)
+            nc.vector.tensor_tensor(near[:, :V], ys[t][:].indirect(l1_t[:]), f1[:], ALU.mult)
+            nc.vector.tensor_tensor(near[:, V:], ys[t][:].indirect(r1_t[:]), c1[:], ALU.mult)
+            return near
 
-        w2c = keep.tile([P, N], U32, name="w2c", tag="y3", align_bytes=64)
-        w2s = keep.tile([P, N], U8, name="w2s", align_bytes=64)
-        zq = [(keep.tile([P, P], U32, name=f"zc{h}", tag=tag, align_bytes=64), keep.tile([P, P], U8, name=f"zs{h}", align_bytes=64)) for h, tag in enumerate(("zc0", "z0"))]
+        def fetch_far(t, h0, h1, near, dbank, ybank, between=None):
+            n = h1 - h0
+            far = buf(f"far{t}_{h0}", P * n)
+            base = nq[:, t, P * h0 : P * h1]
+            nc.scalar.activation(base, ys[t][:].indirect(r2_t[:, 8 * h0 : 8 * h1]), ACT.Copy, scale=-1.0)
+            if between:
+                between()
+            nc.scalar.activation(far[:], ys[t][:].indirect(l2_t[:, 8 * h0 : 8 * h1]), ACT.Copy)
+            dacc = bank(dbank, f"dacc{t}_{h0}")
+            lead = bank(ybank, f"lead{t}_{h0}")
+            for h in range(n):
+                turn(blk(lead, h), blk(near, h0 + h), h == 0, False)
+            for h in range(n):
+                turn(blk(lead, h), blk(near, 2 + h0 + h), False, False)
+            for h in range(n):
+                turn(blk(lead, h), blk(base, h), False, h == n - 1)
+            for h in range(n):
+                turn(blk(dacc, h), blk(base, h), h == 0, False)
+            for h in range(n):
+                turn(blk(dacc, h), blk(far, h), False, h == n - 1)
+            fars.append(far)
+            return t, h0, h1, dacc, lead
 
-        def quantize_w2(cols):
-            nc.vector.quantize_mx(w2c[:, cols].bitcast(FP8X4), w2s[:, cols], w2g[:, cols, :].rearrange("p c j -> p (c j)"))
+        def scale_step(t, h0, h1, dacc, lead):
+            w = P * (h1 - h0)
+            step = buf(f"step{t}_{h0}", w)
+            nc.vector.tensor_tensor(
+                step[:].rearrange("p (g c) -> p g c", c=16),
+                dacc[:, :w].rearrange("p (g c) -> p g c", c=16),
+                f2t[:, 8 * h0 : 8 * h1].unsqueeze(2).to_broadcast([P, 8 * (h1 - h0), 16]),
+                ALU.mult,
+            )
+            return step
 
-        def quantize_z(h, cols):
-            zc, zs = zq[h]
-            nc.vector.quantize_mx(zc[:, cols].bitcast(FP8X4), zs[:, cols], z[h][:, cols, :].rearrange("p v t -> p (v t)"))
+        def larger(sums, step):
+            t, h0, h1, dacc, lead = sums
+            top = buf(f"top{t}_{h0}", P * (h1 - h0))
+            nc.vector.tensor_tensor(top[:], lead[:, : P * (h1 - h0)], step[:], ALU.max)
+            for h in range(h0, h1):
+                turn(blk(zacc[h], t), blk(top, h - h0), True, True)
 
-        nc.vector.scalar_tensor_tensor(second[:, 2, :], n3[:], -1.0, n4[:], ALU.mult, ALU.subtract)
-        quantize_w2(slice(0, 256))
-        nc.vector.scalar_tensor_tensor(second[:, 3, :], m3[:], -1.0, m4[:], ALU.mult, ALU.subtract)
-        quantize_z(0, slice(0, P))
-        quantize_w2(slice(256, 512))
+        def cast_w2(c, tag):
+            g = buf(f"w2g{c}", 2 * PACK * P, BF16, tag=tag)
+            nc.scalar.copy(
+                g[:].rearrange("p (c i j) -> p c j i", i=4, j=PACK),
+                w2raw[:, :, 2 * P * c : 2 * P * (c + 1)].rearrange("p j (c i) -> p c j i", i=4),
+            )
+            return g
+
+        def quantize(name, src, tag=None):
+            codes = buf(name + "c", src.shape[1] // PACK, U32, tag=tag)
+            scales = buf(name + "s", src.shape[1] // PACK, U8)
+            nc.vector.quantize_mx(codes[:].bitcast(FP8X4), scales[:], src)
+            return codes, scales
+
+        def round_z(h, cols):
+            nc.vector.tensor_tensor(
+                z[h][:, cols, :].rearrange("p (c i) t -> p c t i", i=2),
+                zacc[h][:].rearrange("p (t v) -> p t v", t=PACK)[:, :, cols].rearrange("p t (c i) -> p c t i", i=2),
+                nq[:, :, P * h : P * (h + 1)][:, :, cols].rearrange("p t (c i) -> p c t i", i=2),
+                ALU.subtract,
+            )
+
+        near0 = fetch_near(0, None)
+        sums0 = fetch_far(0, 0, 2, near0, 7, 6, between=lambda: nc.scalar.copy(ys[1][:], yacc[1][:]))
+        nc.scalar.copy(f2t[:], f2acc[:, 0:V:16])
+        nc.scalar.copy(ys[2][:], yacc[2][:])
+        near1 = fetch_near(1, None)
+        sums1 = fetch_far(1, 0, 2, near1, 1, 2)
+        larger(sums0, scale_step(*sums0))
+        nc.scalar.copy(ys[3][:], yacc[3][:])
+        near2 = fetch_near(2, "far0_0")
+        sums2 = fetch_far(2, 0, 2, near2, 5, 0)
+        larger(sums1, scale_step(*sums1))
+        near3 = fetch_near(3, "far1_0")
+        sums3 = [fetch_far(3, 0, 1, near3, 7, 6), fetch_far(3, 1, 2, near3, 1, 2)]
+        larger(sums2, scale_step(*sums2))
+        w2g = [cast_w2(0, "top1_0"), cast_w2(1, "step2_0")]
+        for sums in sums3:
+            larger(sums, scale_step(*sums))
+        round_z(0, slice(0, P))
+        w2q = [quantize("w2_0", w2g[0][:], tag="top3_0")]
+        zq = [quantize("z0", z[0][:].rearrange("p v t -> p (v t)"))]
+        zc1 = buf("z1c", P, U32)
+        zs1 = buf("z1s", P, U8)
+        zq.append((zc1, zs1))
         parts = (slice(0, 64), slice(64, P))
         for cols in parts:
-            nc.vector.tensor_tensor(
-                z[1][:, cols, :],
-                zacc[1][:].rearrange("p (t v) -> p v t", t=PACK)[:, cols, :],
-                second[:, :, cols].rearrange("p t v -> p v t"),
-                ALU.max,
-            )
+            round_z(1, cols)
+        w2q.append(quantize("w2_1", w2g[1][:], tag="z0"))
         for cols in parts:
-            quantize_z(1, cols)
-
+            nc.vector.quantize_mx(zc1[:, cols].bitcast(FP8X4), zs1[:, cols], z[1][:, cols, :].rearrange("p v t -> p (v t)"))
 
         outv = out.rearrange("(t p) v -> p t v", t=PACK)
         for h in range(2):
             zc, zs = zq[h]
             res = keep.tile([P, PACK, P], F32, name=f"res{h}")
             if h == 0:
-                pieces = ((6, 0, 2, nc.scalar.copy, nc.sync), (2, 2, 4, nc.scalar.copy, nc.sync))
+                pieces = ((5, 0, 2, nc.scalar.copy, nc.sync), (6, 2, 4, nc.scalar.copy, nc.sync))
             else:
-                pieces = ((7, 0, 2, nc.scalar.copy, nc.sync), (3, 2, 4, nc.vector.tensor_copy, nc.sync))
+                pieces = ((7, 0, 2, nc.scalar.copy, nc.sync), (0, 2, 4, nc.vector.tensor_copy, nc.sync))
             for b, t0, t1, copy, queue in pieces:
                 acc = bank(b, f"oacc{h}_{b}")
                 for t in range(t0, t1):
                     cols = slice(P * t, P * (t + 1))
-                    nc.tensor.matmul_mx(acc[:, cols], w2c[:, cols].bitcast(FP8X4), w2s[:, cols], zc[:].bitcast(FP8X4), zs[:], start=True, stop=True)
+                    nc.tensor.matmul_mx(acc[:, cols], w2q[t // 2][0][:, P * (t % 2) : P * (t % 2 + 1)].bitcast(FP8X4), w2q[t // 2][1][:, P * (t % 2) : P * (t % 2 + 1)], zc[:].bitcast(FP8X4), zs[:], start=True, stop=True)
                 copy(res[:, t0:t1, :], acc[:, P * t0 : P * t1].rearrange("p (t v) -> p t v", v=P))
                 queue.dma_start(outv[:, t0:t1, P * h : P * (h + 1)], res[:, t0:t1, :])

@@ -120,6 +120,7 @@ def tile_picked_roial_none_p_kernel(tc, x_words, x_scales, w1, fr1, fr2, w2, off
         zacc = [bank(3, "zacc0"), bank(4, "zacc1")]
         z = [keep.tile([P, P, PACK], BF16, name=f"z{h}", tag=f"z{h}", align_bytes=64) for h in range(2)]
         fars = []
+        back = [blk(zacc[1], t) for t in range(3)]
 
         def fetch_near(t, tag):
             near = buf(f"near{t}", 2 * V, tag=tag)
@@ -136,13 +137,12 @@ def tile_picked_roial_none_p_kernel(tc, x_words, x_scales, w1, fr1, fr2, w2, off
                 between()
             nc.scalar.activation(far[:], ys[t][:].indirect(l2_t[:, 8 * h0 : 8 * h1]), ACT.Copy)
             dacc = bank(dbank, f"dacc{t}_{h0}")
-            lead = bank(ybank, f"lead{t}_{h0}")
-            for h in range(n):
-                turn(blk(lead, h), blk(near, h0 + h), h == 0, False)
-            for h in range(n):
-                turn(blk(lead, h), blk(near, 2 + h0 + h), False, False)
-            for h in range(n):
-                turn(blk(lead, h), blk(base, h), False, h == n - 1)
+            lead = None
+            if h0 == 0:
+                lead = bank(ybank, f"lead{t}")
+                turn(blk(lead, 0), blk(near, 0), True, False)
+                turn(blk(lead, 0), blk(near, 2), False, False)
+                turn(blk(lead, 0), blk(base, 0), False, True)
             for h in range(n):
                 turn(blk(dacc, h), blk(base, h), h == 0, False)
             for h in range(n):
@@ -163,10 +163,18 @@ def tile_picked_roial_none_p_kernel(tc, x_words, x_scales, w1, fr1, fr2, w2, off
 
         def larger(sums, step):
             t, h0, h1, dacc, lead = sums
-            top = buf(f"top{t}_{h0}", P * (h1 - h0))
-            nc.vector.tensor_tensor(top[:], lead[:, : P * (h1 - h0)], step[:], ALU.max)
-            for h in range(h0, h1):
-                turn(blk(zacc[h], t), blk(top, h - h0), True, True)
+            if h1 == 2:
+                turn(back[t], blk(step, 1 - h0), True, True)
+            if h0 == 0:
+                top = buf(f"top{t}_{h0}", P)
+                nc.vector.tensor_tensor(top[:], lead[:, :P], step[:, :P], ALU.max)
+                turn(blk(zacc[0], t), top[:], True, True)
+
+        first = keep.tile([P, PACK, P], F32, name="first")
+        second = keep.tile([P, PACK, P], F32, name="second")
+
+        def sum_first(t, near):
+            nc.vector.tensor_tensor(first[:, t, :], blk(near, 1), blk(near, 3), ALU.add)
 
         def cast_w2(c, tag):
             g = buf(f"w2g{c}", 2 * PACK * P, BF16, tag=tag)
@@ -197,16 +205,23 @@ def tile_picked_roial_none_p_kernel(tc, x_words, x_scales, w1, fr1, fr2, w2, off
         near1 = fetch_near(1, None)
         sums1 = fetch_far(1, 0, 2, near1, 1, 2)
         larger(sums0, scale_step(*sums0))
+        sum_first(0, near0)
         nc.scalar.copy(ys[3][:], yacc[3][:])
         near2 = fetch_near(2, "far0_0")
         sums2 = fetch_far(2, 0, 2, near2, 5, 0)
         larger(sums1, scale_step(*sums1))
+        sum_first(1, near1)
         near3 = fetch_near(3, "far1_0")
         sums3 = [fetch_far(3, 0, 1, near3, 7, 6), fetch_far(3, 1, 2, near3, 1, 2)]
         larger(sums2, scale_step(*sums2))
-        w2g = [cast_w2(0, "top1_0"), cast_w2(1, "step2_0")]
-        for sums in sums3:
-            larger(sums, scale_step(*sums))
+        sum_first(2, near2)
+        w2g = [cast_w2(0, "step1_0"), cast_w2(1, "step2_0")]
+        larger(sums3[0], scale_step(*sums3[0]))
+        sum_first(3, near3)
+        back.append(bank(2, "back3")[:, :P])
+        larger(sums3[1], scale_step(*sums3[1]))
+        nc.vector.tensor_tensor(second[:, :3, :], zacc[1][:, : 3 * P].rearrange("p (t v) -> p t v", t=3), nq[:, :3, P:], ALU.subtract)
+        nc.vector.tensor_tensor(second[:, 3, :], back[3], nq[:, 3, P:], ALU.subtract)
         round_z(0, slice(0, P))
         w2q = [quantize("w2_0", w2g[0][:], tag="top3_0")]
         zq = [quantize("z0", z[0][:].rearrange("p v t -> p (v t)"))]
@@ -215,7 +230,12 @@ def tile_picked_roial_none_p_kernel(tc, x_words, x_scales, w1, fr1, fr2, w2, off
         zq.append((zc1, zs1))
         parts = (slice(0, 64), slice(64, P))
         for cols in parts:
-            round_z(1, cols)
+            nc.vector.tensor_tensor(
+                z[1][:, cols, :].rearrange("p (c i) t -> p c t i", i=2),
+                first[:, :, cols].rearrange("p t (c i) -> p c t i", i=2),
+                second[:, :, cols].rearrange("p t (c i) -> p c t i", i=2),
+                ALU.max,
+            )
         w2q.append(quantize("w2_1", w2g[1][:], tag="z0"))
         for cols in parts:
             nc.vector.quantize_mx(zc1[:, cols].bitcast(FP8X4), zs1[:, cols], z[1][:, cols, :].rearrange("p v t -> p (v t)"))

@@ -83,7 +83,7 @@ def tile_picked_roial_none_p_kernel(tc, x_words, x_scales, w1, fr1, fr2, w2, off
         for t in range(3):
             quantize_w1(t)
 
-        c1 = keep.tile([P, V], F32, name="c1")
+        c1 = keep.tile([P, V], F32, name="c1", tag="c1")
         nc.vector.tensor_scalar(c1[:], f1[:], -1.0, 1.0, ALU.mult, ALU.add)
 
         def first_product(acc, t, lo, hi):
@@ -170,17 +170,13 @@ def tile_picked_roial_none_p_kernel(tc, x_words, x_scales, w1, fr1, fr2, w2, off
                 nc.vector.tensor_tensor(top[:], lead[:, :P], step[:, :P], ALU.max)
                 turn(blk(zacc[0], t), top[:], True, True)
 
-        first = keep.tile([P, PACK, P], F32, name="first")
         second = keep.tile([P, PACK, P], F32, name="second")
 
-        def sum_first(t, near):
-            nc.vector.tensor_tensor(first[:, t, :], blk(near, 1), blk(near, 3), ALU.add)
-
-        def cast_w2(c, tag):
-            g = buf(f"w2g{c}", 2 * PACK * P, BF16, tag=tag)
-            nc.scalar.copy(
+        def cast_w2(lo, hi, tag, copy):
+            g = buf(f"w2g{lo}", PACK * (hi - lo), BF16, tag=tag)
+            copy(
                 g[:].rearrange("p (c i j) -> p c j i", i=4, j=PACK),
-                w2raw[:, :, 2 * P * c : 2 * P * (c + 1)].rearrange("p j (c i) -> p c j i", i=4),
+                w2raw[:, :, lo:hi].rearrange("p j (c i) -> p c j i", i=4),
             )
             return g
 
@@ -205,38 +201,44 @@ def tile_picked_roial_none_p_kernel(tc, x_words, x_scales, w1, fr1, fr2, w2, off
         near1 = fetch_near(1, None)
         sums1 = fetch_far(1, 0, 2, near1, 1, 2)
         larger(sums0, scale_step(*sums0))
-        sum_first(0, near0)
         nc.scalar.copy(ys[3][:], yacc[3][:])
         near2 = fetch_near(2, "far0_0")
         sums2 = fetch_far(2, 0, 2, near2, 5, 0)
         larger(sums1, scale_step(*sums1))
-        sum_first(1, near1)
+        w2first = cast_w2(0, P, "step0_0", nc.vector.tensor_copy)
         near3 = fetch_near(3, "far1_0")
+        w2q = [quantize("w2_0", w2first[:])]
         sums3 = [fetch_far(3, 0, 1, near3, 7, 6), fetch_far(3, 1, 2, near3, 1, 2)]
+        first = keep.tile([P, PACK, P], F32, name="first", tag="c1")
+        for t, near in enumerate((near0, near1, near2, near3)):
+            nc.gpsimd.tensor_tensor(first[:, t, :], blk(near, 1), blk(near, 3), ALU.add)
         larger(sums2, scale_step(*sums2))
-        sum_first(2, near2)
-        w2g = [cast_w2(0, "step1_0"), cast_w2(1, "step2_0")]
+        w2g = [cast_w2(P, 3 * P, "step1_0", nc.scalar.copy), cast_w2(3 * P, N, "step2_0", nc.scalar.copy)]
         larger(sums3[0], scale_step(*sums3[0]))
-        sum_first(3, near3)
         back.append(bank(2, "back3")[:, :P])
-        larger(sums3[1], scale_step(*sums3[1]))
         nc.vector.tensor_tensor(second[:, :3, :], zacc[1][:, : 3 * P].rearrange("p (t v) -> p t v", t=3), nq[:, :3, P:], ALU.subtract)
-        nc.vector.tensor_tensor(second[:, 3, :], back[3], nq[:, 3, P:], ALU.subtract)
+        larger(sums3[1], scale_step(*sums3[1]))
         round_z(0, slice(0, P))
-        w2q = [quantize("w2_0", w2g[0][:], tag="top3_0")]
+        nc.vector.tensor_tensor(second[:, 3, :], back[3], nq[:, 3, P:], ALU.subtract)
         zq = [quantize("z0", z[0][:].rearrange("p v t -> p (v t)"))]
+        codes, scales = quantize("w2_1", w2g[0][:], tag="step3_1")
+        w2q.extend([(codes[:, :P], scales[:, :P]), (codes[:, P:], scales[:, P:])])
         zc1 = buf("z1c", P, U32)
         zs1 = buf("z1s", P, U8)
         zq.append((zc1, zs1))
         parts = (slice(0, 64), slice(64, P))
-        for cols in parts:
+
+        def larger_rounded(cols):
             nc.vector.tensor_tensor(
                 z[1][:, cols, :].rearrange("p (c i) t -> p c t i", i=2),
                 first[:, :, cols].rearrange("p t (c i) -> p c t i", i=2),
                 second[:, :, cols].rearrange("p t (c i) -> p c t i", i=2),
                 ALU.max,
             )
-        w2q.append(quantize("w2_1", w2g[1][:], tag="z0"))
+
+        larger_rounded(parts[0])
+        w2q.append(quantize("w2_3", w2g[1][:], tag="z0"))
+        larger_rounded(parts[1])
         for cols in parts:
             nc.vector.quantize_mx(zc1[:, cols].bitcast(FP8X4), zs1[:, cols], z[1][:, cols, :].rearrange("p v t -> p (v t)"))
 
@@ -252,6 +254,6 @@ def tile_picked_roial_none_p_kernel(tc, x_words, x_scales, w1, fr1, fr2, w2, off
                 acc = bank(b, f"oacc{h}_{b}")
                 for t in range(t0, t1):
                     cols = slice(P * t, P * (t + 1))
-                    nc.tensor.matmul_mx(acc[:, cols], w2q[t // 2][0][:, P * (t % 2) : P * (t % 2 + 1)].bitcast(FP8X4), w2q[t // 2][1][:, P * (t % 2) : P * (t % 2 + 1)], zc[:].bitcast(FP8X4), zs[:], start=True, stop=True)
+                    nc.tensor.matmul_mx(acc[:, cols], w2q[t][0][:].bitcast(FP8X4), w2q[t][1][:], zc[:].bitcast(FP8X4), zs[:], start=True, stop=True)
                 copy(res[:, t0:t1, :], acc[:, P * t0 : P * t1].rearrange("p (t v) -> p t v", v=P))
                 queue.dma_start(outv[:, t0:t1, P * h : P * (h + 1)], res[:, t0:t1, :])

@@ -205,15 +205,21 @@ def tile_picked_roial_none_p_kernel(tc, x_words, x_scales, w1, fr1, fr2, w2, off
         near2 = fetch_near(2, "far0_0")
         sums2 = fetch_far(2, 0, 2, near2, 5, 0)
         larger(sums1, scale_step(*sums1))
-        w2first = cast_w2(0, P, "step0_0", nc.vector.tensor_copy)
         near3 = fetch_near(3, "far1_0")
-        w2q = [quantize("w2_0", w2first[:])]
         sums3 = [fetch_far(3, 0, 1, near3, 7, 6), fetch_far(3, 1, 2, near3, 1, 2)]
         first = keep.tile([P, PACK, P], F32, name="first", tag="c1")
         for t, near in enumerate((near0, near1, near2, near3)):
             nc.gpsimd.tensor_tensor(first[:, t, :], blk(near, 1), blk(near, 3), ALU.add)
         larger(sums2, scale_step(*sums2))
-        w2g = [cast_w2(P, 3 * P, "step1_0", nc.scalar.copy), cast_w2(3 * P, N, "step2_0", nc.scalar.copy)]
+        w2g = [cast_w2(0, 2 * P, "step1_0", nc.scalar.copy), cast_w2(2 * P, 3 * P, "step2_0", nc.scalar.copy), buf("w2g_last", PACK * P, BF16, tag="near0")]
+        nc.gpsimd.tensor_scalar(
+            w2g[2][:].rearrange("p (c j) -> p c j", j=PACK),
+            w2raw[:, :, 3 * P :].rearrange("p j c -> p c j"),
+            1.0,
+            0.0,
+            ALU.mult,
+            ALU.add,
+        )
         larger(sums3[0], scale_step(*sums3[0]))
         back.append(bank(2, "back3")[:, :P])
         nc.vector.tensor_tensor(second[:, :3, :], zacc[1][:, : 3 * P].rearrange("p (t v) -> p t v", t=3), nq[:, :3, P:], ALU.subtract)
@@ -222,7 +228,8 @@ def tile_picked_roial_none_p_kernel(tc, x_words, x_scales, w1, fr1, fr2, w2, off
         nc.vector.tensor_tensor(second[:, 3, :], back[3], nq[:, 3, P:], ALU.subtract)
         zq = [quantize("z0", z[0][:].rearrange("p v t -> p (v t)"))]
         codes, scales = quantize("w2_1", w2g[0][:], tag="step3_1")
-        w2q.extend([(codes[:, :P], scales[:, :P]), (codes[:, P:], scales[:, P:])])
+        w2q = [(codes[:, :P], scales[:, :P]), (codes[:, P:], scales[:, P:])]
+        w2q.append(quantize("w2_2", w2g[1][:], tag="far3_1"))
         zc1 = buf("z1c", P, U32)
         zs1 = buf("z1s", P, U8)
         zq.append((zc1, zs1))
@@ -237,7 +244,7 @@ def tile_picked_roial_none_p_kernel(tc, x_words, x_scales, w1, fr1, fr2, w2, off
             )
 
         larger_rounded(parts[0])
-        w2q.append(quantize("w2_3", w2g[1][:], tag="z0"))
+        w2q.append(quantize("w2_3", w2g[2][:], tag="z0"))
         larger_rounded(parts[1])
         for cols in parts:
             nc.vector.quantize_mx(zc1[:, cols].bitcast(FP8X4), zs1[:, cols], z[1][:, cols, :].rearrange("p v t -> p (v t)"))

@@ -36,7 +36,7 @@ def tile_picked_roial_none_p_kernel(tc, x_words, x_scales, w1, fr1, fr2, w2, off
             return lt
 
         def load_share(name, src):
-            f = keep.tile([P, V], F32, name=name)
+            f = keep.tile([P, V], F32, name=name, tag=name, align_bytes=64)
             nc.sync.dma_start(f[:], src.rearrange("(p j) v -> p j v", j=PACK)[:, 0, :])
             return f
 
@@ -83,7 +83,7 @@ def tile_picked_roial_none_p_kernel(tc, x_words, x_scales, w1, fr1, fr2, w2, off
         for t in range(3):
             quantize_w1(t)
 
-        c1 = keep.tile([P, V], F32, name="c1", tag="c1")
+        c1 = keep.tile([P, V], F32, name="c1", tag="c1", align_bytes=64)
         nc.vector.tensor_scalar(c1[:], f1[:], -1.0, 1.0, ALU.mult, ALU.add)
 
         def first_product(acc, t, lo, hi):
@@ -117,68 +117,51 @@ def tile_picked_roial_none_p_kernel(tc, x_words, x_scales, w1, fr1, fr2, w2, off
         f2t = keep.tile([P, 16], F32, name="f2t")
 
         nq = keep.tile([P, PACK, V], F32, name="nq")
-        zacc = [bank(3, "zacc0"), bank(4, "zacc1")]
         z = [keep.tile([P, P, PACK], BF16, name=f"z{h}", tag=f"z{h}", align_bytes=64) for h in range(2)]
+        nears = []
+        allnear = keep.tile([P, PACK, 2 * V], F32, name="allnear")
         fars = []
-        back = [blk(zacc[1], t) for t in range(3)]
 
-        def fetch_near(t, tag):
-            near = buf(f"near{t}", 2 * V, tag=tag)
+        def fetch_near(t, lead):
+            near = allnear[:, t, :]
             nc.vector.tensor_tensor(near[:, :V], ys[t][:].indirect(l1_t[:]), f1[:], ALU.mult)
             nc.vector.tensor_tensor(near[:, V:], ys[t][:].indirect(r1_t[:]), c1[:], ALU.mult)
-            return near
+            nears.append(near)
+            turn(lead, blk(near, 0), t % 2 == 0, False)
+            turn(lead, blk(near, 2), False, False)
 
-        def fetch_far(t, h0, h1, near, dbank, ybank, between=None):
+        def fetch_base(t, h0, h1):
+            nc.scalar.activation(nq[:, t, P * h0 : P * h1], ys[t][:].indirect(r2_t[:, 8 * h0 : 8 * h1]), ACT.Copy, scale=-1.0)
+
+        def fetch_far(t, h0, h1, diff, lead):
             n = h1 - h0
             far = buf(f"far{t}_{h0}", P * n)
             base = nq[:, t, P * h0 : P * h1]
-            nc.scalar.activation(base, ys[t][:].indirect(r2_t[:, 8 * h0 : 8 * h1]), ACT.Copy, scale=-1.0)
-            if between:
-                between()
             nc.scalar.activation(far[:], ys[t][:].indirect(l2_t[:, 8 * h0 : 8 * h1]), ACT.Copy)
-            dacc = bank(dbank, f"dacc{t}_{h0}")
-            lead = None
             if h0 == 0:
-                lead = bank(ybank, f"lead{t}")
-                turn(blk(lead, 0), blk(near, 0), True, False)
-                turn(blk(lead, 0), blk(near, 2), False, False)
-                turn(blk(lead, 0), blk(base, 0), False, True)
+                turn(lead, blk(base, 0), False, t % 2 == 1)
             for h in range(n):
-                turn(blk(dacc, h), blk(base, h), h == 0, False)
+                turn(blk(diff, h), blk(base, h), h == 0, False)
             for h in range(n):
-                turn(blk(dacc, h), blk(far, h), False, h == n - 1)
+                turn(blk(diff, h), blk(far, h), False, h == n - 1)
             fars.append(far)
-            return t, h0, h1, dacc, lead
 
-        def scale_step(t, h0, h1, dacc, lead):
-            w = P * (h1 - h0)
-            step = buf(f"step{t}_{h0}", w)
+        def scale_step(name, diff, tiles, h0, h1):
+            g = 8 * (h1 - h0)
+            step = buf(name, tiles * 16 * g)
             nc.vector.tensor_tensor(
-                step[:].rearrange("p (g c) -> p g c", c=16),
-                dacc[:, :w].rearrange("p (g c) -> p g c", c=16),
-                f2t[:, 8 * h0 : 8 * h1].unsqueeze(2).to_broadcast([P, 8 * (h1 - h0), 16]),
+                step[:].rearrange("p (t g c) -> p t g c", t=tiles, c=16),
+                diff.rearrange("p (t g c) -> p t g c", t=tiles, c=16),
+                f2t[:, 8 * h0 : 8 * h1].unsqueeze(1).unsqueeze(3).to_broadcast([P, tiles, g, 16]),
                 ALU.mult,
             )
             return step
 
-        def larger(sums, step):
-            t, h0, h1, dacc, lead = sums
-            if h1 == 2:
-                turn(back[t], blk(step, 1 - h0), True, True)
-            if h0 == 0:
-                top = buf(f"top{t}_{h0}", P)
-                nc.vector.tensor_tensor(top[:], lead[:, :P], step[:, :P], ALU.max)
-                turn(blk(zacc[0], t), top[:], True, True)
-
-        second = keep.tile([P, PACK, P], F32, name="second")
-
-        def cast_w2(lo, hi, tag, copy):
-            g = buf(f"w2g{lo}", PACK * (hi - lo), BF16, tag=tag)
-            copy(
-                g[:].rearrange("p (c i j) -> p c j i", i=4, j=PACK),
-                w2raw[:, :, lo:hi].rearrange("p j (c i) -> p c j i", i=4),
-            )
-            return g
+        def larger(t0, tiles, lead, step):
+            top = buf(f"top{t0}", tiles * P)
+            nc.vector.tensor_tensor(top[:].rearrange("p (t v) -> p t v", t=tiles), lead.rearrange("p (t v) -> p t v", t=tiles), step, ALU.max)
+            for t in range(tiles):
+                turn(blk(zacc0, t0 + t), blk(top, t), True, True)
 
         def quantize(name, src, tag=None):
             codes = buf(name + "c", src.shape[1] // PACK, U32, tag=tag)
@@ -186,66 +169,88 @@ def tile_picked_roial_none_p_kernel(tc, x_words, x_scales, w1, fr1, fr2, w2, off
             nc.vector.quantize_mx(codes[:].bitcast(FP8X4), scales[:], src)
             return codes, scales
 
-        def round_z(h, cols):
-            nc.vector.tensor_tensor(
-                z[h][:, cols, :].rearrange("p (c i) t -> p c t i", i=2),
-                zacc[h][:].rearrange("p (t v) -> p t v", t=PACK)[:, :, cols].rearrange("p t (c i) -> p c t i", i=2),
-                nq[:, :, P * h : P * (h + 1)][:, :, cols].rearrange("p t (c i) -> p c t i", i=2),
-                ALU.subtract,
-            )
+        def pairs(view):
+            return view.rearrange("p t (c i) -> p c t i", i=2)
 
-        near0 = fetch_near(0, None)
-        sums0 = fetch_far(0, 0, 2, near0, 7, 6, between=lambda: nc.scalar.copy(ys[1][:], yacc[1][:]))
+        diff01 = bank(7, "diff01")
+        lead01 = bank(6, "lead01")
+        fetch_near(0, blk(lead01, 0))
+        fetch_base(0, 0, 2)
+        nc.scalar.copy(ys[1][:], yacc[1][:])
+        fetch_far(0, 0, 2, diff01[:, :V], blk(lead01, 0))
         nc.scalar.copy(f2t[:], f2acc[:, 0:V:16])
         nc.scalar.copy(ys[2][:], yacc[2][:])
-        near1 = fetch_near(1, None)
-        sums1 = fetch_far(1, 0, 2, near1, 1, 2)
-        larger(sums0, scale_step(*sums0))
+        fetch_near(1, blk(lead01, 1))
+        fetch_base(1, 0, 2)
         nc.scalar.copy(ys[3][:], yacc[3][:])
-        near2 = fetch_near(2, "far0_0")
-        sums2 = fetch_far(2, 0, 2, near2, 5, 0)
-        larger(sums1, scale_step(*sums1))
-        near3 = fetch_near(3, "far1_0")
-        sums3 = [fetch_far(3, 0, 1, near3, 7, 6), fetch_far(3, 1, 2, near3, 1, 2)]
-        first = keep.tile([P, PACK, P], F32, name="first", tag="c1")
-        for t, near in enumerate((near0, near1, near2, near3)):
-            nc.gpsimd.tensor_tensor(first[:, t, :], blk(near, 1), blk(near, 3), ALU.add)
-        larger(sums2, scale_step(*sums2))
-        w2g = [cast_w2(0, 2 * P, "step1_0", nc.scalar.copy), cast_w2(2 * P, 3 * P, "step2_0", nc.scalar.copy), buf("w2g_last", PACK * P, BF16, tag="near0")]
+        fetch_far(1, 0, 2, diff01[:, V:], blk(lead01, 1))
+        lead23 = bank(0, "lead23")
+        fetch_near(2, blk(lead23, 0))
+        fetch_near(3, blk(lead23, 1))
+        w2lo = buf("w2lo", 2 * PACK * P, BF16, tag="c1")
         nc.gpsimd.tensor_scalar(
-            w2g[2][:].rearrange("p (c j) -> p c j", j=PACK),
-            w2raw[:, :, 3 * P :].rearrange("p j c -> p c j"),
+            w2lo[:].rearrange("p (c j) -> p c j", j=PACK),
+            w2raw[:, :, : 2 * P].rearrange("p j c -> p c j"),
             1.0,
             0.0,
             ALU.mult,
             ALU.add,
         )
-        larger(sums3[0], scale_step(*sums3[0]))
-        back.append(bank(2, "back3")[:, :P])
-        nc.vector.tensor_tensor(second[:, :3, :], zacc[1][:, : 3 * P].rearrange("p (t v) -> p t v", t=3), nq[:, :3, P:], ALU.subtract)
-        larger(sums3[1], scale_step(*sums3[1]))
-        round_z(0, slice(0, P))
-        nc.vector.tensor_tensor(second[:, 3, :], back[3], nq[:, 3, P:], ALU.subtract)
+        first = keep.tile([P, P, PACK], BF16, name="first", align_bytes=64)
+        for cols in (slice(0, 64), slice(64, P)):
+            nc.gpsimd.tensor_tensor(
+                first[:, cols, :],
+                allnear[:, :, P:V][:, :, cols].rearrange("p t v -> p v t"),
+                allnear[:, :, V + P :][:, :, cols].rearrange("p t v -> p v t"),
+                ALU.add,
+            )
+        diff23 = [bank(2, "diff23_0"), bank(5, "diff23_1")]
+        for t in (2, 3):
+            fetch_base(t, 0, 1)
+            fetch_far(t, 0, 1, blk(diff23[0], t - 2), blk(lead23, t - 2))
+        zacc0 = bank(3, "zacc0")
+        step01 = scale_step("step01", diff01[:], 2, 0, 2)
+        larger(0, 2, lead01[:, :V], step01[:].rearrange("p (t v) -> p t v", t=2)[:, :, :P])
+        back = bank(4, "back")
+        second = keep.tile([P, P, PACK], BF16, name="second", align_bytes=64)
+        for t in range(2):
+            turn(blk(back, t), blk(step01, 2 * t + 1), True, True)
+        for t in (2, 3):
+            fetch_base(t, 1, 2)
+            fetch_far(t, 1, 2, blk(diff23[1], t - 2), None)
+        w2hi = buf("w2hi", 2 * PACK * P, BF16, tag="far2_0")
+        nc.scalar.copy(
+            w2hi[:].rearrange("p (c i j) -> p c j i", i=4, j=PACK),
+            w2raw[:, :, 2 * P :].rearrange("p j (c i) -> p c j i", i=4),
+        )
+        step23 = scale_step("step23_0", diff23[0][:, :V], 2, 0, 1)
+        w2q = [quantize("w2_lo", w2lo[:])]
+        larger(2, 2, lead23[:, :V], step23[:].rearrange("p (t v) -> p t v", t=2))
+        step23 = scale_step("step23_1", diff23[1][:, :V], 2, 1, 2)
+        nc.vector.tensor_tensor(
+            z[0][:].rearrange("p (c i) t -> p c t i", i=2),
+            pairs(zacc0[:].rearrange("p (t v) -> p t v", t=PACK)),
+            pairs(nq[:, :, :P]),
+            ALU.subtract,
+        )
+        for t in range(2):
+            turn(blk(back, 2 + t), blk(step23, t), True, True)
+        parts = (slice(0, 64), slice(64, P))
+
         zq = [quantize("z0", z[0][:].rearrange("p v t -> p (v t)"))]
-        codes, scales = quantize("w2_1", w2g[0][:], tag="step3_1")
-        w2q = [(codes[:, :P], scales[:, :P]), (codes[:, P:], scales[:, P:])]
-        w2q.append(quantize("w2_2", w2g[1][:], tag="far3_1"))
+        for cols in parts:
+            nc.vector.tensor_tensor(
+                second[:, cols, :].rearrange("p (c i) t -> p c t i", i=2),
+                pairs(back[:].rearrange("p (t v) -> p t v", t=PACK)[:, :, cols]),
+                pairs(nq[:, :, P:][:, :, cols]),
+                ALU.subtract,
+            )
+        w2q.append(quantize("w2_hi", w2hi[:], tag="z0"))
+        for cols in parts:
+            nc.vector.tensor_tensor(z[1][:, cols, :], first[:, cols, :], second[:, cols, :], ALU.max)
         zc1 = buf("z1c", P, U32)
         zs1 = buf("z1s", P, U8)
         zq.append((zc1, zs1))
-        parts = (slice(0, 64), slice(64, P))
-
-        def larger_rounded(cols):
-            nc.vector.tensor_tensor(
-                z[1][:, cols, :].rearrange("p (c i) t -> p c t i", i=2),
-                first[:, :, cols].rearrange("p t (c i) -> p c t i", i=2),
-                second[:, :, cols].rearrange("p t (c i) -> p c t i", i=2),
-                ALU.max,
-            )
-
-        larger_rounded(parts[0])
-        w2q.append(quantize("w2_3", w2g[2][:], tag="z0"))
-        larger_rounded(parts[1])
         for cols in parts:
             nc.vector.quantize_mx(zc1[:, cols].bitcast(FP8X4), zs1[:, cols], z[1][:, cols, :].rearrange("p v t -> p (v t)"))
 
@@ -254,13 +259,13 @@ def tile_picked_roial_none_p_kernel(tc, x_words, x_scales, w1, fr1, fr2, w2, off
             zc, zs = zq[h]
             res = keep.tile([P, PACK, P], F32, name=f"res{h}")
             if h == 0:
-                pieces = ((5, 0, 2, nc.scalar.copy, nc.sync), (6, 2, 4, nc.scalar.copy, nc.sync))
+                pieces = ((7, 0, 2, nc.scalar.copy, nc.sync), (6, 2, 4, nc.scalar.copy, nc.sync))
             else:
-                pieces = ((7, 0, 2, nc.scalar.copy, nc.sync), (0, 2, 4, nc.vector.tensor_copy, nc.sync))
+                pieces = ((2, 0, 2, nc.scalar.copy, nc.sync), (0, 2, 4, nc.vector.tensor_copy, nc.sync))
             for b, t0, t1, copy, queue in pieces:
                 acc = bank(b, f"oacc{h}_{b}")
                 for t in range(t0, t1):
                     cols = slice(P * t, P * (t + 1))
-                    nc.tensor.matmul_mx(acc[:, cols], w2q[t][0][:].bitcast(FP8X4), w2q[t][1][:], zc[:].bitcast(FP8X4), zs[:], start=True, stop=True)
+                    nc.tensor.matmul_mx(acc[:, cols], w2q[t // 2][0][:, P * (t % 2) : P * (t % 2 + 1)].bitcast(FP8X4), w2q[t // 2][1][:, P * (t % 2) : P * (t % 2 + 1)], zc[:].bitcast(FP8X4), zs[:], start=True, stop=True)
                 copy(res[:, t0:t1, :], acc[:, P * t0 : P * t1].rearrange("p (t v) -> p t v", v=P))
                 queue.dma_start(outv[:, t0:t1, P * h : P * (h + 1)], res[:, t0:t1, :])

@@ -187,15 +187,6 @@ def tile_picked_roial_none_p_kernel(tc, x_words, x_scales, w1, fr1, fr2, w2, off
         lead23 = bank(0, "lead23")
         fetch_near(2, blk(lead23, 0))
         fetch_near(3, blk(lead23, 1))
-        w2lo = buf("w2lo", 2 * PACK * P, BF16, tag="c1")
-        nc.gpsimd.tensor_scalar(
-            w2lo[:].rearrange("p (c j) -> p c j", j=PACK),
-            w2raw[:, :, : 2 * P].rearrange("p j c -> p c j"),
-            1.0,
-            0.0,
-            ALU.mult,
-            ALU.add,
-        )
         first = keep.tile([P, P, PACK], BF16, name="first", align_bytes=64)
         for cols in (slice(0, 64), slice(64, P)):
             nc.gpsimd.tensor_tensor(
@@ -218,13 +209,13 @@ def tile_picked_roial_none_p_kernel(tc, x_words, x_scales, w1, fr1, fr2, w2, off
         for t in (2, 3):
             fetch_base(t, 1, 2)
             fetch_far(t, 1, 2, blk(diff23[1], t - 2), None)
-        w2hi = buf("w2hi", 2 * PACK * P, BF16, tag="far2_0")
-        nc.scalar.copy(
-            w2hi[:].rearrange("p (c i j) -> p c j i", i=4, j=PACK),
-            w2raw[:, :, 2 * P :].rearrange("p j (c i) -> p c j i", i=4),
-        )
+        w2g = [buf("w2lo", 2 * PACK * P, BF16, tag="far2_0"), buf("w2hi", 2 * PACK * P, BF16, tag="far3_0")]
+        for c in range(2):
+            nc.scalar.copy(
+                w2g[c][:].rearrange("p (c i j) -> p c j i", i=4, j=PACK),
+                w2raw[:, :, 2 * P * c : 2 * P * (c + 1)].rearrange("p j (c i) -> p c j i", i=4),
+            )
         step23 = scale_step("step23_0", diff23[0][:, :V], 2, 0, 1)
-        w2q = [quantize("w2_lo", w2lo[:])]
         larger(2, 2, lead23[:, :V], step23[:].rearrange("p (t v) -> p t v", t=2))
         step23 = scale_step("step23_1", diff23[1][:, :V], 2, 1, 2)
         nc.vector.tensor_tensor(
@@ -237,6 +228,7 @@ def tile_picked_roial_none_p_kernel(tc, x_words, x_scales, w1, fr1, fr2, w2, off
             turn(blk(back, 2 + t), blk(step23, t), True, True)
         parts = (slice(0, 64), slice(64, P))
 
+        w2q = [quantize("w2_lo", w2g[0][:], tag="top2")]
         zq = [quantize("z0", z[0][:].rearrange("p v t -> p (v t)"))]
         for cols in parts:
             nc.vector.tensor_tensor(
@@ -245,7 +237,7 @@ def tile_picked_roial_none_p_kernel(tc, x_words, x_scales, w1, fr1, fr2, w2, off
                 pairs(nq[:, :, P:][:, :, cols]),
                 ALU.subtract,
             )
-        w2q.append(quantize("w2_hi", w2hi[:], tag="z0"))
+        w2q.append(quantize("w2_hi", w2g[1][:], tag="z0"))
         for cols in parts:
             nc.vector.tensor_tensor(z[1][:, cols, :], first[:, cols, :], second[:, cols, :], ALU.max)
         zc1 = buf("z1c", P, U32)

@@ -210,11 +210,19 @@ def tile_picked_roial_none_p_kernel(tc, x_words, x_scales, w1, fr1, fr2, w2, off
             fetch_base(t, 1, 2)
             fetch_far(t, 1, 2, blk(diff23[1], t - 2), None)
         w2g = [buf("w2lo", 2 * PACK * P, BF16, tag="far2_0"), buf("w2hi", 2 * PACK * P, BF16, tag="far3_0")]
-        for c in range(2):
+        for g, lo, hi in ((w2g[0][:], 0, 2 * P), (w2g[1][:, : PACK * P], 2 * P, 3 * P)):
             nc.scalar.copy(
-                w2g[c][:].rearrange("p (c i j) -> p c j i", i=4, j=PACK),
-                w2raw[:, :, 2 * P * c : 2 * P * (c + 1)].rearrange("p j (c i) -> p c j i", i=4),
+                g.rearrange("p (c i j) -> p c j i", i=4, j=PACK),
+                w2raw[:, :, lo:hi].rearrange("p j (c i) -> p c j i", i=4),
             )
+        nc.gpsimd.tensor_scalar(
+            w2g[1][:, PACK * P :].rearrange("p (c j) -> p c j", j=PACK),
+            w2raw[:, :, 3 * P :].rearrange("p j c -> p c j"),
+            1.0,
+            0.0,
+            ALU.mult,
+            ALU.add,
+        )
         step23 = scale_step("step23_0", diff23[0][:, :V], 2, 0, 1)
         larger(2, 2, lead23[:, :V], step23[:].rearrange("p (t v) -> p t v", t=2))
         step23 = scale_step("step23_1", diff23[1][:, :V], 2, 1, 2)

from contextlib import ExitStack

import concourse.mybir as mybir
from concourse.masks import make_identity

K, T, S, V, N, H = 512, 2048, 512, 256, 512, 512
FLOPS = 2 * K * H * S + 2 * H * N * V

F32 = mybir.dt.float32
BF16 = mybir.dt.bfloat16
I32 = mybir.dt.int32
U32 = mybir.dt.uint32
U16 = mybir.dt.uint16
U8 = mybir.dt.uint8
FP8X4 = mybir.dt.float8_e4m3fn_x4
ALU = mybir.AluOpType
ACT = mybir.ActivationFunctionType

P = 128
PACK = 4
BANK = 512


def tile_picked_roial_none_p_kernel(tc, x_words, x_scales, w1, fr1, fr2, w2, offs, l1, r1, l2, r2, out):
    nc = tc.nc
    with ExitStack() as ctx:
        keep = ctx.enter_context(tc.tile_pool(name="keep", bufs=1))
        psum = ctx.enter_context(tc.psum_pool(name="psum", bufs=1))

        def bank(b, name):
            return psum.tile([P, BANK], F32, name=name, tag=f"bank{b}")

        def load_list(name, src):
            lt = keep.tile([P, src.shape[1]], U16, name="list_" + name)
            nc.sync.dma_start(lt[:], src)
            return lt

        def load_share(name, src):
            f = keep.tile([P, V], F32, name=name, tag=name, align_bytes=64)
            nc.sync.dma_start(f[:], src.rearrange("(p j) v -> p j v", j=PACK)[:, 0, :])
            return f

        offs_t = load_list("offs", offs)
        xw = keep.tile([P, T], I32, name="xw", align_bytes=64)
        nc.sync.dma_start(xw[:], x_words[0].rearrange("p n t -> p (n t)").bitcast(I32))
        l1_t = load_list("l1", l1)
        r1_t = load_list("r1", r1)
        xs = keep.tile([P, T], U8, name="xs", align_bytes=64)
        nc.vector.memset(xs[:].bitcast(I32), 0)
        for r in range(4):
            nc.sync.dma_start(xs[r:P:32, :].bitcast(I32), x_scales[0, r:16:4, :].bitcast(I32))
        w1raw = keep.tile([P, PACK, H], F32, name="w1raw")
        nc.sync.dma_start(w1raw[:], w1.rearrange("(p j) c -> p j c", j=PACK))
        f1 = load_share("f1", fr1)
        f2 = load_share("f2", fr2)
        l2_t = load_list("l2", l2)
        r2_t = load_list("r2", r2)
        w2raw = keep.tile([P, PACK, N], F32, name="w2raw")
        w2rows = w2.rearrange("(q t i) c -> t q i c", t=PACK, i=4)
        for t in range(PACK):
            nc.sync.dma_start(w2raw[:, t, :], w2rows[t])

        ident = keep.tile([P, P], F32, name="ident")
        make_identity(nc, ident[:])

        xq_w = keep.tile([P, S], U32, name="xq_w", align_bytes=64)
        nc.vector.tensor_copy(xq_w[:], xw[:].bitcast(U32).indirect(offs_t[:]))
        xq_s = keep.tile([P, S], U8, name="xq_s", align_bytes=64)
        nc.vector.tensor_copy(xq_s[:], xs[:].indirect(offs_t[:]))

        w1cols = w1raw[:].rearrange("p j (q t i) -> p t q j i", t=PACK, i=4)
        w1g = [keep.tile([P, P, PACK], BF16, name=f"w1g{t}", align_bytes=64) for t in range(PACK)]
        for t in range(2):
            nc.vector.tensor_copy(w1g[t][:].rearrange("p (q i) j -> p q j i", i=4), w1cols[:, t])
        for t in range(2, PACK):
            nc.scalar.copy(w1g[t][:].rearrange("p (q i) j -> p q j i", i=4), w1cols[:, t])
        w1c = [keep.tile([P, P], U32, name=f"w1c{t}", align_bytes=64) for t in range(PACK)]
        w1s = [keep.tile([P, P], U8, name=f"w1s{t}", align_bytes=64) for t in range(PACK)]

        def quantize_w1(t):
            nc.vector.quantize_mx(w1c[t][:].bitcast(FP8X4), w1s[t][:], w1g[t][:].rearrange("p m j -> p (m j)"))

        for t in range(3):
            quantize_w1(t)

        c1 = keep.tile([P, V], F32, name="c1", tag="c1", align_bytes=64)
        nc.vector.tensor_scalar(c1[:], f1[:], -1.0, 1.0, ALU.mult, ALU.add)

        def first_product(acc, t, lo, hi):
            nc.tensor.matmul_mx(acc[:, lo:hi], w1c[t][:].bitcast(FP8X4), w1s[t][:], xq_w[:, lo:hi].bitcast(FP8X4), xq_s[:, lo:hi], start=True, stop=True)

        ys = [keep.tile([P, S], F32, name=f"y{t}", tag=f"y{t}", align_bytes=64) for t in range(PACK)]
        for b, lo, hi, copy in ((0, 0, 256, nc.vector.tensor_copy), (1, 256, 384, nc.scalar.copy), (2, 384, 512, nc.scalar.copy)):
            acc = bank(b, f"yacc0_{b}")
            first_product(acc, 0, lo, hi)
            copy(ys[0][:, lo:hi], acc[:, lo:hi])
        quantize_w1(3)
        yacc = [None]
        for t in range(1, PACK):
            acc = bank(2 + t, f"yacc{t}")
            first_product(acc, t, 0, 256)
            first_product(acc, t, 256, 512)
            yacc.append(acc)

        def turn(dst, src, start, stop):
            nc.tensor.matmul(dst, src, ident[:], start=start, stop=stop, is_transpose=True)

        def blk(g, b):
            return g[:, P * b : P * (b + 1)]

        def buf(name, width, dtype=F32, tag=None):
            return keep.tile([P, width], dtype, name=name, tag=tag or name, align_bytes=64)

        f2acc = bank(1, "f2acc")
        for h in range(2):
            turn(blk(f2acc, h), blk(f2, h), True, True)
        f2t = keep.tile([P, 16], F32, name="f2t")

        nq = keep.tile([P, PACK, V], F32, name="nq")
        z = [keep.tile([P, P, PACK], BF16, name=f"z{h}", tag=f"z{h}", align_bytes=64) for h in range(2)]
        nears = []
        allnear = keep.tile([P, PACK, 2 * V], F32, name="allnear")
        fars = []

        def fetch_near(t, lead):
            near = allnear[:, t, :]
            nc.vector.tensor_tensor(near[:, :V], ys[t][:].indirect(l1_t[:]), f1[:], ALU.mult)
            nc.vector.tensor_tensor(near[:, V:], ys[t][:].indirect(r1_t[:]), c1[:], ALU.mult)
            nears.append(near)
            turn(lead, blk(near, 0), t % 2 == 0, False)
            turn(lead, blk(near, 2), False, False)

        def fetch_base(t, h0, h1):
            nc.scalar.activation(nq[:, t, P * h0 : P * h1], ys[t][:].indirect(r2_t[:, 8 * h0 : 8 * h1]), ACT.Copy, scale=-1.0)

        def fetch_far(t, h0, h1, diff, lead):
            n = h1 - h0
            far = buf(f"far{t}_{h0}", P * n)
            base = nq[:, t, P * h0 : P * h1]
            nc.scalar.activation(far[:], ys[t][:].indirect(l2_t[:, 8 * h0 : 8 * h1]), ACT.Copy)
            if h0 == 0:
                turn(lead, blk(base, 0), False, t % 2 == 1)
            for h in range(n):
                turn(blk(diff, h), blk(base, h), h == 0, False)
            for h in range(n):
                turn(blk(diff, h), blk(far, h), False, h == n - 1)
            fars.append(far)

        def scale_step(name, diff, tiles, h0, h1):
            g = 8 * (h1 - h0)
            step = buf(name, tiles * 16 * g)
            nc.vector.tensor_tensor(
                step[:].rearrange("p (t g c) -> p t g c", t=tiles, c=16),
                diff.rearrange("p (t g c) -> p t g c", t=tiles, c=16),
                f2t[:, 8 * h0 : 8 * h1].unsqueeze(1).unsqueeze(3).to_broadcast([P, tiles, g, 16]),
                ALU.mult,
            )
            return step

        def larger(t0, tiles, lead, step):
            top = buf(f"top{t0}", tiles * P)
            nc.vector.tensor_tensor(top[:].rearrange("p (t v) -> p t v", t=tiles), lead.rearrange("p (t v) -> p t v", t=tiles), step, ALU.max)
            for t in range(tiles):
                turn(blk(zacc0, t0 + t), blk(top, t), True, True)

        def quantize(name, src, tag=None):
            codes = buf(name + "c", src.shape[1] // PACK, U32, tag=tag)
            scales = buf(name + "s", src.shape[1] // PACK, U8)
            nc.vector.quantize_mx(codes[:].bitcast(FP8X4), scales[:], src)
            return codes, scales

        def pairs(view):
            return view.rearrange("p t (c i) -> p c t i", i=2)

        diff01 = bank(7, "diff01")
        lead01 = bank(6, "lead01")
        fetch_near(0, blk(lead01, 0))
        fetch_base(0, 0, 2)
        nc.scalar.copy(ys[1][:], yacc[1][:])
        fetch_far(0, 0, 2, diff01[:, :V], blk(lead01, 0))
        nc.scalar.copy(f2t[:], f2acc[:, 0:V:16])
        nc.scalar.copy(ys[2][:], yacc[2][:])
        fetch_near(1, blk(lead01, 1))
        fetch_base(1, 0, 2)
        nc.scalar.copy(ys[3][:], yacc[3][:])
        fetch_far(1, 0, 2, diff01[:, V:], blk(lead01, 1))
        lead23 = bank(0, "lead23")
        fetch_near(2, blk(lead23, 0))
        fetch_near(3, blk(lead23, 1))
        first = keep.tile([P, P, PACK], BF16, name="first", align_bytes=64)
        for cols in (slice(0, 64), slice(64, P)):
            nc.gpsimd.tensor_tensor(
                first[:, cols, :],
                allnear[:, :, P:V][:, :, cols].rearrange("p t v -> p v t"),
                allnear[:, :, V + P :][:, :, cols].rearrange("p t v -> p v t"),
                ALU.add,
            )
        diff23 = [bank(2, "diff23_0"), bank(5, "diff23_1")]
        for t in (2, 3):
            fetch_base(t, 0, 1)
            fetch_far(t, 0, 1, blk(diff23[0], t - 2), blk(lead23, t - 2))
        zacc0 = bank(3, "zacc0")
        step01 = scale_step("step01", diff01[:], 2, 0, 2)
        larger(0, 2, lead01[:, :V], step01[:].rearrange("p (t v) -> p t v", t=2)[:, :, :P])
        back = bank(4, "back")
        second = keep.tile([P, P, PACK], BF16, name="second", align_bytes=64)
        for t in range(2):
            turn(blk(back, t), blk(step01, 2 * t + 1), True, True)
        for t in (2, 3):
            fetch_base(t, 1, 2)
            fetch_far(t, 1, 2, blk(diff23[1], t - 2), None)
        w2g = [buf("w2lo", 2 * PACK * P, BF16, tag="far2_0"), buf("w2hi", 2 * PACK * P, BF16, tag="far3_0")]
        for g, lo, hi in ((w2g[0][:], 0, 2 * P), (w2g[1][:, : PACK * P], 2 * P, 3 * P)):
            nc.scalar.copy(
                g.rearrange("p (c i j) -> p c j i", i=4, j=PACK),
                w2raw[:, :, lo:hi].rearrange("p j (c i) -> p c j i", i=4),
            )
        nc.gpsimd.tensor_scalar(
            w2g[1][:, PACK * P :].rearrange("p (c j) -> p c j", j=PACK),
            w2raw[:, :, 3 * P :].rearrange("p j c -> p c j"),
            1.0,
            0.0,
            ALU.mult,
            ALU.add,
        )
        step23 = scale_step("step23_0", diff23[0][:, :V], 2, 0, 1)
        larger(2, 2, lead23[:, :V], step23[:].rearrange("p (t v) -> p t v", t=2))
        step23 = scale_step("step23_1", diff23[1][:, :V], 2, 1, 2)
        nc.vector.tensor_tensor(
            z[0][:].rearrange("p (c i) t -> p c t i", i=2),
            pairs(zacc0[:].rearrange("p (t v) -> p t v", t=PACK)),
            pairs(nq[:, :, :P]),
            ALU.subtract,
        )
        for t in range(2):
            turn(blk(back, 2 + t), blk(step23, t), True, True)
        parts = (slice(0, 64), slice(64, P))

        w2q = [quantize("w2_lo", w2g[0][:], tag="top2")]
        zq = [quantize("z0", z[0][:].rearrange("p v t -> p (v t)"))]
        for cols in parts:
            nc.vector.tensor_tensor(
                second[:, cols, :].rearrange("p (c i) t -> p c t i", i=2),
                pairs(back[:].rearrange("p (t v) -> p t v", t=PACK)[:, :, cols]),
                pairs(nq[:, :, P:][:, :, cols]),
                ALU.subtract,
            )
        w2q.append(quantize("w2_hi", w2g[1][:], tag="z0"))
        for cols in parts:
            nc.vector.tensor_tensor(z[1][:, cols, :], first[:, cols, :], second[:, cols, :], ALU.max)
        zc1 = buf("z1c", P, U32)
        zs1 = buf("z1s", P, U8)
        zq.append((zc1, zs1))
        for cols in parts:
            nc.vector.quantize_mx(zc1[:, cols].bitcast(FP8X4), zs1[:, cols], z[1][:, cols, :].rearrange("p v t -> p (v t)"))

        outv = out.rearrange("(t p) v -> p t v", t=PACK)
        for h in range(2):
            zc, zs = zq[h]
            res = keep.tile([P, PACK, P], F32, name=f"res{h}")
            if h == 0:
                pieces = ((7, 0, 2, nc.scalar.copy, nc.sync), (6, 2, 4, nc.scalar.copy, nc.sync))
            else:
                pieces = ((2, 0, 2, nc.scalar.copy, nc.sync), (0, 2, 4, nc.vector.tensor_copy, nc.sync))
            for b, t0, t1, copy, queue in pieces:
                acc = bank(b, f"oacc{h}_{b}")
                for t in range(t0, t1):
                    cols = slice(P * t, P * (t + 1))
                    nc.tensor.matmul_mx(acc[:, cols], w2q[t // 2][0][:, P * (t % 2) : P * (t % 2 + 1)].bitcast(FP8X4), w2q[t // 2][1][:, P * (t % 2) : P * (t % 2 + 1)], zc[:].bitcast(FP8X4), zs[:], start=True, stop=True)
                copy(res[:, t0:t1, :], acc[:, P * t0 : P * t1].rearrange("p (t v) -> p t v", v=P))
                queue.dma_start(outv[:, t0:t1, P * h : P * (h + 1)], res[:, t0:t1, :])
